import numpy as np
import ml_dtypes


def mxq(x, axis, fmt="e4m3"):
    dtype, down = {"e4m3": (ml_dtypes.float8_e4m3fn, 7), "e5m2": (ml_dtypes.float8_e5m2, 14)}[fmt]
    v = np.moveaxis(np.asarray(x, np.float32).astype(ml_dtypes.bfloat16).astype(np.float64), axis, -1)
    blocks = v.reshape(v.shape[:-1] + (-1, 32))
    amax = np.abs(blocks).max(-1, keepdims=True)
    byte = np.maximum(np.where(amax > 0, np.frexp(amax)[1] - 1 + 127, 0) - down, 1)
    scale = np.exp2(byte - 127.0)
    codes = (blocks / scale).astype(np.float32).astype(dtype).astype(np.float64)
    return np.moveaxis((codes * scale).reshape(v.shape), -1, axis)


WIDE = False


def mx_kscale(k):
    if not WIDE:
        return np.ones(k)
    levels = np.array([10, -10, 5, -5, 0])
    if k % 512:
        return np.exp2(np.random.permutation(np.resize(levels, k // 32))).repeat(32)
    a = np.empty((k // 512, 16))
    for p in range(k // 512):
        a[p, :8] = np.random.permutation(np.resize(levels, 8))
        for g in range(8):
            far = levels[np.abs(levels - a[p, g]) >= 10]
            a[p, g + 8] = far[np.random.randint(len(far))]
    return np.exp2(a.ravel()).repeat(32)


BF16 = ml_dtypes.bfloat16


def bf(x):
    return np.asarray(x, np.float32).astype(BF16)


def f64(x):
    return np.asarray(x).astype(np.float64)

def planes(Y):
    n, m = Y.shape
    b = f64(bf(Y)).reshape(n // 32, 32, m)
    amax = np.abs(b).max(1)
    byte = np.clip(np.where(amax > 0, np.frexp(amax)[1] - 1 + 127 - 7, 1), 1, 254)
    codes = (b * np.exp2(127.0 - byte)[:, None, :]).reshape(n, m).astype(np.float32).astype(ml_dtypes.float8_e4m3fn).view(np.uint8)
    words = codes.reshape(n // 512, 128, 4, m).transpose(0, 1, 3, 2)
    return np.ascontiguousarray(words), np.ascontiguousarray(byte.astype(np.uint8).reshape(n // 512, 16, m))


B, T, A, E = 2, 1024, 256, 512
F = 2 * A
EPS = 1e-6


def dpfp_features(x):
    p = np.maximum(np.concatenate([x, -x], axis=-1), 0.0)
    r = p * np.roll(p, 1, axis=-1)
    return r / np.sqrt(np.mean(r * r, axis=-1, keepdims=True) + EPS)


def setup_inputs():
    t = mx_kscale(T)
    u = mx_kscale(F)
    return {
        "q": bf(np.random.standard_normal((B, T, A)) * 0.08),
        "k": bf(np.random.standard_normal((B, T, A)) * 0.08),
        "v": bf(np.random.standard_normal((B, T, E)) / t[None, :, None]),
        "beta": bf(np.random.standard_normal((B, T)) * t[None, :]),
        "s0": bf(np.random.standard_normal((B, F, E))),
        "gq": bf(np.random.standard_normal(F) * u),
        "gs": bf((1.0 + 0.1 * np.random.standard_normal(F)) / u),
    }


def core(q, k, v, beta, s0, gq, gs):
    t_len = k.shape[1]
    f_dim = s0.shape[1]
    kw = dpfp_features(f64(k)) * f64(beta)[:, :, None]
    d = (mxq(kw, 1, "e4m3").transpose(0, 2, 1) @ mxq(f64(v), 1, "e4m3")) / np.sqrt(t_len)
    s = (0.7 * f64(s0) + d) * f64(gs)[None, :, None]
    qf = dpfp_features(f64(q)) * f64(gq)[None, None, :]
    return (mxq(qf, 2, "e4m3") @ mxq(s, 1, "e4m3")) / np.sqrt(f_dim)


def reference(q, k, v, beta, s0, gq, gs):
    R_out = core(q, k, v, beta, s0, gq, gs)
    words, scales = planes(np.moveaxis(R_out, 2, 0).reshape(512, -1))
    return R_out, words, scales

@@ -1,0 +1,285 @@
+from contextlib import ExitStack
+
+import concourse.mybir as mybir
+from concourse.masks import make_identity
+
+B, T, A, E = 2, 1024, 256, 512
+F = 2 * A
+FLOPS = 2 * 2 * B * T * F * E
+
+F32 = mybir.dt.float32
+BF16 = mybir.dt.bfloat16
+I32 = mybir.dt.int32
+U32 = mybir.dt.uint32
+U8 = mybir.dt.uint8
+FP8X4 = mybir.dt.float8_e4m3fn_x4
+ALU = mybir.AluOpType
+ACT = mybir.ActivationFunctionType
+P = 128
+
+
+def tile_dpfpfastweightwriteread_x1_kernel(tc, q, k, v, beta, s0, gq, gs, out_0, out_1, out_2):
+    nc = tc.nc
+
+    with ExitStack() as ctx:
+        keep = ctx.enter_context(tc.tile_pool(name="keep", bufs=1))
+        work = ctx.enter_context(tc.tile_pool(name="work", bufs=2))
+        small = ctx.enter_context(tc.tile_pool(name="small", bufs=2))
+        outp = ctx.enter_context(tc.tile_pool(name="outp", bufs=4))
+        psum_d = ctx.enter_context(tc.psum_pool(name="psum_d", bufs=2))
+        psum_q = ctx.enter_context(tc.psum_pool(name="psum_q", bufs=2))
+        psum_o = ctx.enter_context(tc.psum_pool(name="psum_o", bufs=4))
+
+        kx, qx, vx, s0x = {}, {}, {}, {}
+        beta_sb = keep.tile([P, B * 2 * 4], BF16, name="beta_sb")
+        gs_sb = keep.tile([P, 4], BF16, name="gs_sb")
+        gqb = keep.tile([P, F], BF16, name="gqb")
+
+        def load_k(b, g):
+            kx[b, g] = keep.tile([P, 4, A], BF16, name="kx%d%d" % (b, g))
+            nc.sync.dma_start(out=kx[b, g][:], in_=k[b, 512 * g : 512 * g + 512, :].rearrange("(p j) a -> p j a", j=4))
+
+        def load_q(b, h):
+            qx[b, h] = keep.tile([P, 4, A], BF16, name="qx%d%d" % (b, h))
+            nc.sync.dma_start(out=qx[b, h][:], in_=q[b, 512 * h : 512 * h + 512, :].rearrange("(c p) a -> p c a", p=P))
+
+        def load_v(b, g):
+            vx[b, g] = keep.tile([P, 4, E], BF16, name="vx%d%d" % (b, g))
+            nc.sync.dma_start(out=vx[b, g][:], in_=v[b, 512 * g : 512 * g + 512, :].rearrange("(p j) e -> p j e", j=4))
+
+        def load_s0(b):
+            s0x[b] = keep.tile([P, 4, E], BF16, name="s0x%d" % b)
+            nc.sync.dma_start(out=s0x[b][:], in_=s0[b].rearrange("(p j) e -> p j e", j=4))
+
+        load_k(0, 0)
+        nc.scalar.dma_start(
+            out=beta_sb[:].rearrange("p (r j) -> p r j", j=4),
+            in_=beta.rearrange("b (g p j) -> p (b g) j", g=2, j=4),
+        )
+        nc.scalar.dma_start(out=gs_sb[:], in_=gs.rearrange("(p j) -> p j", j=4))
+        nc.scalar.dma_start(out=gqb[:], in_=gq.partition_broadcast(P))
+        load_k(0, 1)
+        load_q(0, 0)
+        load_q(0, 1)
+        load_v(0, 0)
+        load_v(0, 1)
+        load_s0(0)
+        for h in (0, 1):
+            load_k(1, h)
+        for h in (0, 1):
+            load_q(1, h)
+        for h in (0, 1):
+            load_v(1, h)
+        load_s0(1)
+
+        ident = keep.tile([P, P], F32, name="ident")
+        make_identity(nc, ident[:])
+
+        gs07 = keep.tile([P, 4], F32, name="gs07")
+        gs32 = keep.tile([P, 4], F32, name="gs32")
+        nc.vector.tensor_scalar(out=gs07[:], in0=gs_sb[:], scalar1=0.7, scalar2=None, op0=ALU.mult)
+        nc.vector.tensor_scalar(out=gs32[:], in0=gs_sb[:], scalar1=1.0 / 32.0, scalar2=None, op0=ALU.mult)
+
+        def products(x, w):
+            nc.vector.tensor_tensor(out=w[:, :, 1:A], in0=x[:, :, 1:A], in1=x[:, :, 0 : A - 1], op=ALU.mult)
+            nc.vector.scalar_tensor_tensor(
+                out=w[:, :, 0:1], in0=x[:, :, 0:1], scalar=-1.0, in1=x[:, :, A - 1 : A], op0=ALU.mult, op1=ALU.mult
+            )
+
+        def squares(u, ss, base):
+            for j in range(4):
+                junk = small.tile([P, A], BF16, name="junk")
+                nc.scalar.activation(
+                    out=junk[:], in_=u[:, j, :], func=ACT.Square, accum_out=ss[:, base + j : base + j + 1]
+                )
+
+        def inv_rms(ss, name):
+            ms = small.tile([P, 8], F32, name="ms")
+            nc.vector.tensor_scalar(
+                out=ms[:], in0=ss[:], scalar1=1.0 / F, scalar2=1e-6, op0=ALU.mult, op1=ALU.add
+            )
+            rt = small.tile([P, 8], F32, name="rt")
+            nc.scalar.activation(out=rt[:], in_=ms[:], func=ACT.Sqrt)
+            r = small.tile([P, 8], F32, name=name)
+            nc.vector.reciprocal(out=r[:], in_=rt[:])
+            return r
+
+        for b in range(B):
+            ssk = small.tile([P, 8], F32, name="ssk")
+            wk = {}
+            for g in range(2):
+                wk[g] = work.tile([P, 4, A], F32, name="wk%d" % g)
+                products(kx[b, g], wk[g])
+                nc.scalar.activation(out=wk[g][:], in_=wk[g][:], func=ACT.Relu)
+                squares(wk[g], ssk, 4 * g)
+            rk = inv_rms(ssk, "rk")
+            ck = small.tile([P, 8], F32, name="ck")
+            nc.vector.tensor_tensor(out=ck[:], in0=rk[:], in1=beta_sb[:, 8 * b : 8 * b + 8], op=ALU.mult)
+
+            ssq = small.tile([P, 8], F32, name="ssq")
+            uq = {}
+            for h in range(2):
+                uq[h] = work.tile([P, 4, A], F32, name="uq%d" % h)
+                products(qx[b, h], uq[h])
+                nc.scalar.activation(out=uq[h][:], in_=uq[h][:], func=ACT.Relu)
+                squares(uq[h], ssq, 4 * h)
+            rq = inv_rms(ssq, "rq")
+
+            kc = work.tile([P, 2, F], U32, name="kc", align_bytes=64)
+            ks = work.tile([P, 2, F], U8, name="ks", align_bytes=64)
+            vc = work.tile([P, 2, E], U32, name="vc", align_bytes=64)
+            vs = work.tile([P, 2, E], U8, name="vs", align_bytes=64)
+            for g in range(2):
+                xi = work.tile([P, 4, 64, 4], BF16, name="xi")
+                nc.scalar.copy(out=xi[:], in_=kx[b, g][:].rearrange("p j (m t) -> p t m j", t=4))
+                mi = work.tile([P, 4, 256], BF16, name="mi")
+                nc.vector.tensor_scalar(
+                    out=mi[:], in0=xi[:].rearrange("p t m j -> p t (m j)"), scalar1=0.0, scalar2=None, op0=ALU.is_gt
+                )
+                vi = work.tile([P, E, 4], BF16, name="vi", align_bytes=64)
+                if b == 0 and g == 1:
+                    nc.scalar.copy(out=vi[:], in_=vx[b, g][:].rearrange("p j e -> p e j"))
+                else:
+                    nc.vector.tensor_copy(out=vi[:], in_=vx[b, g][:].rearrange("p j e -> p e j"))
+                kr = work.tile([P, 4, A], BF16, name="kr")
+                for j in range(4):
+                    nc.vector.tensor_scalar(
+                        out=kr[:, j, :],
+                        in0=wk[g][:, j, :],
+                        scalar1=ck[:, 4 * g + j : 4 * g + j + 1],
+                        scalar2=None,
+                        op0=ALU.mult,
+                    )
+                nc.vector.quantize_mx(
+                    out=vc[:, g, :].bitcast(FP8X4), scales=vs[:, g, :], in_=vi[:].rearrange("p e j -> p (e j)")
+                )
+                ki = work.tile([P, 4, 64, 4], BF16, name="ki")
+                nc.vector.tensor_copy(out=ki[:], in_=kr[:].rearrange("p j (m t) -> p t m j", t=4))
+                kw = work.tile([P, 4, 2, 256], BF16, name="kw", align_bytes=64)
+                ki4 = ki[:].rearrange("p t m j -> p t (m j)")
+                nc.vector.tensor_tensor(out=kw[:, :, 0, :], in0=ki4, in1=mi[:], op=ALU.mult)
+                nc.vector.tensor_tensor(out=kw[:, :, 1, :], in0=ki4, in1=kw[:, :, 0, :], op=ALU.subtract)
+                nc.vector.quantize_mx(
+                    out=kc[:, g, :].bitcast(FP8X4), scales=ks[:, g, :], in_=kw[:].rearrange("p t h c -> p (t h c)")
+                )
+
+            s0p = work.tile([P, 4, E], F32, name="s0p")
+            sn = work.tile([P, 4, E], BF16, name="sn")
+            for t in range(4):
+                nc.scalar.activation(out=s0p[:, t, :], in_=s0x[b][:, t, :], func=ACT.Copy, scale=gs07[:, t : t + 1])
+                d = psum_d.tile([P, E], F32, name="d")
+                for g in range(2):
+                    cols = slice(P * t, P * t + P)
+                    nc.tensor.matmul_mx(
+                        out=d[:],
+                        lhsT=kc[:, g, cols].bitcast(FP8X4),
+                        lhsT_scale=ks[:, g, cols],
+                        rhs=vc[:, g, :].bitcast(FP8X4),
+                        rhs_scale=vs[:, g, :],
+                        start=(g == 0),
+                        stop=(g == 1),
+                    )
+                nc.vector.scalar_tensor_tensor(
+                    out=sn[:, t, :], in0=d[:], scalar=gs32[:, t : t + 1], in1=s0p[:, t, :], op0=ALU.mult, op1=ALU.add
+                )
+            si = work.tile([P, 4, P, 4], BF16, name="si", align_bytes=64)
+            nc.vector.tensor_copy(out=si[:], in_=sn[:].rearrange("p j (m t) -> p t m j", t=4))
+            sc = work.tile([P, E], U32, name="sc", align_bytes=64)
+            sscale = work.tile([P, E], U8, name="sscale", align_bytes=64)
+            nc.vector.quantize_mx(
+                out=sc[:].bitcast(FP8X4), scales=sscale[:], in_=si[:].rearrange("p t m j -> p (t m j)")
+            )
+
+            qc = work.tile([P, T], U32, name="qc", align_bytes=64)
+            qs = work.tile([P, T], U8, name="qs", align_bytes=64)
+            ysc = work.tile([P, T], U8, name="ysc", align_bytes=64)
+            for h in range(2):
+                qm = work.tile([P, 4, 2, A], BF16, name="qm")
+                nc.vector.tensor_scalar(out=qm[:, :, 0, :], in0=qx[b, h][:], scalar1=0.0, scalar2=None, op0=ALU.is_gt)
+                nc.vector.tensor_scalar(out=qm[:, :, 1, :], in0=qx[b, h][:], scalar1=0.0, scalar2=None, op0=ALU.is_lt)
+                z = work.tile([P, 4, F], BF16, name="z")
+                nc.vector.tensor_tensor(
+                    out=z[:],
+                    in0=qm[:].rearrange("p c h a -> p c (h a)"),
+                    in1=gqb[:].unsqueeze(1).to_broadcast([P, 4, F]),
+                    op=ALU.mult,
+                )
+                for cc in range(2):
+                    qf = work.tile([P, 2, F], BF16, name="qf")
+                    qt = psum_q.tile([P, 2, 2, P], F32, name="qt")
+                    for ci in range(2):
+                        c = 2 * cc + ci
+                        nc.vector.scalar_tensor_tensor(
+                            out=qf[:, ci, :].rearrange("p (h a) -> p h a", h=2),
+                            in0=uq[h][:, c, :].unsqueeze(1).to_broadcast([P, 2, A]),
+                            scalar=rq[:, 4 * h + c : 4 * h + c + 1],
+                            in1=z[:, c, :].rearrange("p (h a) -> p h a", h=2),
+                            op0=ALU.mult,
+                            op1=ALU.mult,
+                        )
+                        words = qf[:, ci, :].bitcast(F32)
+                        for u in range(2):
+                            nc.tensor.transpose(qt[:, ci, u, :], words[:, u:A:2], ident[:])
+                    qg = work.tile([P, 2, P, 4], BF16, name="qg", align_bytes=64)
+                    nc.scalar.copy(
+                        out=qg[:].rearrange("p c r e -> p (c r e)").bitcast(F32).rearrange("p (c r u) -> p c r u", c=2, u=2),
+                        in_=qt[:].rearrange("p c u r -> p c r u"),
+                    )
+                    tok2 = slice(512 * h + 256 * cc, 512 * h + 256 * cc + 256)
+                    nc.vector.quantize_mx(
+                        out=qc[:, tok2].bitcast(FP8X4), scales=qs[:, tok2], in_=qg[:].rearrange("p c r e -> p (c r e)")
+                    )
+                    yg = work.tile([P, 256, 4], BF16, name="yg", align_bytes=64)
+                    for n in range(2):
+                        r0 = 512 * h + 256 * cc + P * n
+                        tok = slice(r0, r0 + P)
+                        y = psum_o.tile([P, 4, P], F32, name="o")
+                        for t in range(4):
+                            cols = slice(P * t, P * t + P)
+                            nc.tensor.matmul_mx(
+                                out=y[:, t, :],
+                                lhsT=sc[:, cols].bitcast(FP8X4),
+                                lhsT_scale=sscale[:, cols],
+                                rhs=qc[:, tok].bitcast(FP8X4),
+                                rhs_scale=qs[:, tok],
+                                start=True,
+                                stop=True,
+                            )
+                        nc.scalar.activation(
+                            out=yg[:, P * n : P * n + P, :],
+                            in_=y[:].rearrange("p t r -> p r t"),
+                            func=ACT.Copy,
+                            scale=F**-0.5,
+                        )
+                        o = psum_o.tile([P, E], F32, name="o")
+                        nc.tensor.matmul_mx(
+                            out=o[:],
+                            lhsT=qc[:, tok].bitcast(FP8X4),
+                            lhsT_scale=qs[:, tok],
+                            rhs=sc[:].bitcast(FP8X4),
+                            rhs_scale=sscale[:],
+                            start=True,
+                            stop=True,
+                        )
+                        ot = outp.tile([P, E], F32, name="ot")
+                        o_in = o[:].rearrange("p (t m) -> p m t", t=4)
+                        o_out = ot[:].rearrange("p (m t) -> p m t", t=4)
+                        if b == 1 and h == 1:
+                            nc.vector.tensor_scalar(out=o_out, in0=o_in, scalar1=F**-0.5, scalar2=None, op0=ALU.mult)
+                        else:
+                            nc.scalar.activation(out=o_out, in_=o_in, func=ACT.Copy, scale=F**-0.5)
+                        nc.sync.dma_start(out=out_0[b, tok, :], in_=ot[:])
+                    yc = work.tile([P, 256], U32, name="yc", align_bytes=64)
+                    nc.vector.quantize_mx(
+                        out=yc[:].bitcast(FP8X4), scales=ysc[:, tok2], in_=yg[:].rearrange("p r t -> p (r t)")
+                    )
+                    m0 = T * b + 512 * h + 256 * cc
+                    nc.sync.dma_start(
+                        out=out_1[0, :, m0 : m0 + 256, :].rearrange("p m t -> p (m t)").bitcast(I32),
+                        in_=yc[:].bitcast(I32),
+                    )
+            for quad in range(4):
+                nc.sync.dma_start(
+                    out=out_2[0, 4 * quad : 4 * quad + 4, T * b : T * b + T].bitcast(I32),
+                    in_=ysc[32 * quad : 32 * quad + 4, :].bitcast(I32),
+                )

@@ -25,15 +25,27 @@ def tile_dpfpfastweightwriteread_x1_kernel(tc, q, k, v, beta, s0, gq, gs, out_0,
         keep = ctx.enter_context(tc.tile_pool(name="keep", bufs=1))
         work = ctx.enter_context(tc.tile_pool(name="work", bufs=2))
         small = ctx.enter_context(tc.tile_pool(name="small", bufs=2))
-        outp = ctx.enter_context(tc.tile_pool(name="outp", bufs=4))
+        outp = ctx.enter_context(tc.tile_pool(name="outp", bufs=6))
         psum_d = ctx.enter_context(tc.psum_pool(name="psum_d", bufs=2))
         psum_q = ctx.enter_context(tc.psum_pool(name="psum_q", bufs=2))
         psum_o = ctx.enter_context(tc.psum_pool(name="psum_o", bufs=4))
+        ctx.enter_context(tc.manual_schedule())
 
         kx, qx, vx, s0x = {}, {}, {}, {}
+        wk, uq, ssk, ssq, ck, rq = {}, {}, {}, {}, {}, {}
+        xi, mi, vi, kr, ki, kw, kc, ks, vc, vs = {}, {}, {}, {}, {}, {}, {}, {}, {}, {}
+        vp = {}
+        s0p, sn, si, sc, sscale = {}, {}, {}, {}, {}
+        qm, z, qf, qt, qg, qc, qs, yg, ysc, dd = {}, {}, {}, {}, {}, {}, {}, {}, {}, {}
+
         beta_sb = keep.tile([P, B * 2 * 4], BF16, name="beta_sb")
         gs_sb = keep.tile([P, 4], BF16, name="gs_sb")
         gqb = keep.tile([P, F], BF16, name="gqb")
+        neg_half = keep.tile([P, 8], F32, name="neg_half")
+        ident = keep.tile([P, P], F32, name="ident")
+        ident16 = keep.tile([P, P], BF16, name="ident16")
+        gs07 = keep.tile([P, 4], F32, name="gs07")
+        gs32 = keep.tile([P, 4], F32, name="gs32")
 
         def load_k(b, g):
             kx[b, g] = keep.tile([P, 4, A], BF16, name="kx%d%d" % (b, g))
@@ -51,34 +63,24 @@ def tile_dpfpfastweightwriteread_x1_kernel(tc, q, k, v, beta, s0, gq, gs, out_0,
             s0x[b] = keep.tile([P, 4, E], BF16, name="s0x%d" % b)
             nc.sync.dma_start(out=s0x[b][:], in_=s0[b].rearrange("(p j) e -> p j e", j=4))
 
-        load_k(0, 0)
-        nc.scalar.dma_start(
-            out=beta_sb[:].rearrange("p (r j) -> p r j", j=4),
-            in_=beta.rearrange("b (g p j) -> p (b g) j", g=2, j=4),
-        )
-        nc.scalar.dma_start(out=gs_sb[:], in_=gs.rearrange("(p j) -> p j", j=4))
-        nc.scalar.dma_start(out=gqb[:], in_=gq.partition_broadcast(P))
-        load_k(0, 1)
-        load_q(0, 0)
-        load_q(0, 1)
-        load_v(0, 0)
-        load_v(0, 1)
-        load_s0(0)
-        for h in (0, 1):
-            load_k(1, h)
-        for h in (0, 1):
-            load_q(1, h)
-        for h in (0, 1):
-            load_v(1, h)
-        load_s0(1)
+        def load_small():
+            nc.scalar.dma_start(
+                out=beta_sb[:].rearrange("p (r j) -> p r j", j=4),
+                in_=beta.rearrange("b (g p j) -> p (b g) j", g=2, j=4),
+            )
+            nc.scalar.dma_start(out=gs_sb[:], in_=gs.rearrange("(p j) -> p j", j=4))
+            nc.scalar.dma_start(out=gqb[:], in_=gq.partition_broadcast(P))
 
-        ident = keep.tile([P, P], F32, name="ident")
-        make_identity(nc, ident[:])
+        def consts():
+            nc.gpsimd.memset(neg_half[:], -0.5)
+            make_identity(nc, ident[:])
+            make_identity(nc, ident16[:])
 
-        gs07 = keep.tile([P, 4], F32, name="gs07")
-        gs32 = keep.tile([P, 4], F32, name="gs32")
-        nc.vector.tensor_scalar(out=gs07[:], in0=gs_sb[:], scalar1=0.7, scalar2=None, op0=ALU.mult)
-        nc.vector.tensor_scalar(out=gs32[:], in0=gs_sb[:], scalar1=1.0 / 32.0, scalar2=None, op0=ALU.mult)
+        def gains():
+            nc.gpsimd.tensor_scalar(out=gs07[:], in0=gs_sb[:], scalar1=0.7, scalar2=0.0, op0=ALU.mult, op1=ALU.add)
+            nc.gpsimd.tensor_scalar(
+                out=gs32[:], in0=gs_sb[:], scalar1=1.0 / 32.0, scalar2=0.0, op0=ALU.mult, op1=ALU.add
+            )
 
         def products(x, w):
             nc.vector.tensor_tensor(out=w[:, :, 1:A], in0=x[:, :, 1:A], in1=x[:, :, 0 : A - 1], op=ALU.mult)
@@ -86,200 +88,516 @@ def tile_dpfpfastweightwriteread_x1_kernel(tc, q, k, v, beta, s0, gq, gs, out_0,
                 out=w[:, :, 0:1], in0=x[:, :, 0:1], scalar=-1.0, in1=x[:, :, A - 1 : A], op0=ALU.mult, op1=ALU.mult
             )
 
-        def squares(u, ss, base):
+        def squares(w, ss, base):
+            nc.scalar.activation(out=w[:], in_=w[:], func=ACT.Relu)
             for j in range(4):
                 junk = small.tile([P, A], BF16, name="junk")
                 nc.scalar.activation(
-                    out=junk[:], in_=u[:, j, :], func=ACT.Square, accum_out=ss[:, base + j : base + j + 1]
+                    out=junk[:], in_=w[:, j, :], func=ACT.Square, accum_out=ss[:, base + j : base + j + 1]
                 )
 
-        def inv_rms(ss, name):
+        def inv_rms(ss, r):
             ms = small.tile([P, 8], F32, name="ms")
+            nc.gpsimd.tensor_scalar(out=ms[:], in0=ss[:], scalar1=1.0 / F, scalar2=1e-6, op0=ALU.mult, op1=ALU.add)
+            nc.gpsimd.tensor_tensor(out=r[:], in0=ms[:], in1=neg_half[:], op=ALU.pow)
+
+        def WK(b, g):
+            wk[b, g] = work.tile([P, 4, A], F32, name="wk%d" % g)
+            products(kx[b, g], wk[b, g])
+
+        def RK(b, g):
+            if b not in ssk:
+                ssk[b] = small.tile([P, 8], F32, name="ssk")
+            squares(wk[b, g], ssk[b], 4 * g)
+
+        def CK(b):
+            rk = small.tile([P, 8], F32, name="rk")
+            inv_rms(ssk[b], rk)
+            ck[b] = small.tile([P, 8], F32, name="ck")
+            nc.gpsimd.tensor_tensor(out=ck[b][:], in0=rk[:], in1=beta_sb[:, 8 * b : 8 * b + 8], op=ALU.mult)
+
+        def WQ(b, h):
+            uq[b, h] = work.tile([P, 4, A], F32, name="uq%d" % h)
+            products(qx[b, h], uq[b, h])
+
+        def RQ(b, h):
+            if b not in ssq:
+                ssq[b] = small.tile([P, 8], F32, name="ssq")
+            squares(uq[b, h], ssq[b], 4 * h)
+
+        def CQ(b):
+            rq[b] = small.tile([P, 8], F32, name="rq")
+            inv_rms(ssq[b], rq[b])
+
+        def XI(b, g, eng):
+            xi[b, g] = work.tile([P, 4, 64, 4], BF16, name="xi")
+            src = kx[b, g][:].rearrange("p j (m t) -> p t m j", t=4)
+            if eng == "S":
+                nc.scalar.copy(out=xi[b, g][:], in_=src)
+            else:
+                nc.vector.tensor_copy(out=xi[b, g][:], in_=src)
+
+        def MI(b, g):
+            mi[b, g] = work.tile([P, 4, 256], BF16, name="mi")
             nc.vector.tensor_scalar(
-                out=ms[:], in0=ss[:], scalar1=1.0 / F, scalar2=1e-6, op0=ALU.mult, op1=ALU.add
+                out=mi[b, g][:],
+                in0=xi[b, g][:].rearrange("p t m j -> p t (m j)"),
+                scalar1=0.0,
+                scalar2=None,
+                op0=ALU.is_gt,
             )
-            rt = small.tile([P, 8], F32, name="rt")
-            nc.scalar.activation(out=rt[:], in_=ms[:], func=ACT.Sqrt)
-            r = small.tile([P, 8], F32, name=name)
-            nc.vector.reciprocal(out=r[:], in_=rt[:])
-            return r
 
-        for b in range(B):
-            ssk = small.tile([P, 8], F32, name="ssk")
-            wk = {}
-            for g in range(2):
-                wk[g] = work.tile([P, 4, A], F32, name="wk%d" % g)
-                products(kx[b, g], wk[g])
-                nc.scalar.activation(out=wk[g][:], in_=wk[g][:], func=ACT.Relu)
-                squares(wk[g], ssk, 4 * g)
-            rk = inv_rms(ssk, "rk")
-            ck = small.tile([P, 8], F32, name="ck")
-            nc.vector.tensor_tensor(out=ck[:], in0=rk[:], in1=beta_sb[:, 8 * b : 8 * b + 8], op=ALU.mult)
+        def VI(b, g, eng):
+            vi[b, g] = work.tile([P, E, 4], BF16, name="vi", align_bytes=64, bufs=3)
+            if eng == "S":
+                nc.scalar.copy(out=vi[b, g][:], in_=vx[b, g][:].rearrange("p j e -> p e j"))
+            else:
+                nc.vector.tensor_copy(out=vi[b, g][:], in_=vx[b, g][:].rearrange("p j e -> p e j"))
 
-            ssq = small.tile([P, 8], F32, name="ssq")
-            uq = {}
-            for h in range(2):
-                uq[h] = work.tile([P, 4, A], F32, name="uq%d" % h)
-                products(qx[b, h], uq[h])
-                nc.scalar.activation(out=uq[h][:], in_=uq[h][:], func=ACT.Relu)
-                squares(uq[h], ssq, 4 * h)
-            rq = inv_rms(ssq, "rq")
-
-            kc = work.tile([P, 2, F], U32, name="kc", align_bytes=64)
-            ks = work.tile([P, 2, F], U8, name="ks", align_bytes=64)
-            vc = work.tile([P, 2, E], U32, name="vc", align_bytes=64)
-            vs = work.tile([P, 2, E], U8, name="vs", align_bytes=64)
-            for g in range(2):
-                xi = work.tile([P, 4, 64, 4], BF16, name="xi")
-                nc.scalar.copy(out=xi[:], in_=kx[b, g][:].rearrange("p j (m t) -> p t m j", t=4))
-                mi = work.tile([P, 4, 256], BF16, name="mi")
-                nc.vector.tensor_scalar(
-                    out=mi[:], in0=xi[:].rearrange("p t m j -> p t (m j)"), scalar1=0.0, scalar2=None, op0=ALU.is_gt
-                )
-                vi = work.tile([P, E, 4], BF16, name="vi", align_bytes=64)
-                if b == 0 and g == 1:
-                    nc.scalar.copy(out=vi[:], in_=vx[b, g][:].rearrange("p j e -> p e j"))
-                else:
-                    nc.vector.tensor_copy(out=vi[:], in_=vx[b, g][:].rearrange("p j e -> p e j"))
-                kr = work.tile([P, 4, A], BF16, name="kr")
-                for j in range(4):
-                    nc.vector.tensor_scalar(
-                        out=kr[:, j, :],
-                        in0=wk[g][:, j, :],
-                        scalar1=ck[:, 4 * g + j : 4 * g + j + 1],
-                        scalar2=None,
-                        op0=ALU.mult,
-                    )
-                nc.vector.quantize_mx(
-                    out=vc[:, g, :].bitcast(FP8X4), scales=vs[:, g, :], in_=vi[:].rearrange("p e j -> p (e j)")
-                )
-                ki = work.tile([P, 4, 64, 4], BF16, name="ki")
-                nc.vector.tensor_copy(out=ki[:], in_=kr[:].rearrange("p j (m t) -> p t m j", t=4))
-                kw = work.tile([P, 4, 2, 256], BF16, name="kw", align_bytes=64)
-                ki4 = ki[:].rearrange("p t m j -> p t (m j)")
-                nc.vector.tensor_tensor(out=kw[:, :, 0, :], in0=ki4, in1=mi[:], op=ALU.mult)
-                nc.vector.tensor_tensor(out=kw[:, :, 1, :], in0=ki4, in1=kw[:, :, 0, :], op=ALU.subtract)
-                nc.vector.quantize_mx(
-                    out=kc[:, g, :].bitcast(FP8X4), scales=ks[:, g, :], in_=kw[:].rearrange("p t h c -> p (t h c)")
+        def VP(b, g, r):
+            vp[b, g, r] = psum_o.tile([P, 2 * E], BF16, name="o")
+            src = vx[b, g][:].rearrange("p j e -> p e j")
+            for i in range(2):
+                e0 = 256 * r + 128 * i
+                nc.tensor.matmul(
+                    out=vp[b, g, r][:, E * i : E * i + E],
+                    lhsT=ident16[:],
+                    rhs=src[:, e0 : e0 + 128, :],
+                    start=True,
+                    stop=True,
                 )
 
-            s0p = work.tile([P, 4, E], F32, name="s0p")
-            sn = work.tile([P, 4, E], BF16, name="sn")
-            for t in range(4):
-                nc.scalar.activation(out=s0p[:, t, :], in_=s0x[b][:, t, :], func=ACT.Copy, scale=gs07[:, t : t + 1])
-                d = psum_d.tile([P, E], F32, name="d")
-                for g in range(2):
-                    cols = slice(P * t, P * t + P)
-                    nc.tensor.matmul_mx(
-                        out=d[:],
-                        lhsT=kc[:, g, cols].bitcast(FP8X4),
-                        lhsT_scale=ks[:, g, cols],
-                        rhs=vc[:, g, :].bitcast(FP8X4),
-                        rhs_scale=vs[:, g, :],
-                        start=(g == 0),
-                        stop=(g == 1),
-                    )
-                nc.vector.scalar_tensor_tensor(
-                    out=sn[:, t, :], in0=d[:], scalar=gs32[:, t : t + 1], in1=s0p[:, t, :], op0=ALU.mult, op1=ALU.add
-                )
-            si = work.tile([P, 4, P, 4], BF16, name="si", align_bytes=64)
-            nc.vector.tensor_copy(out=si[:], in_=sn[:].rearrange("p j (m t) -> p t m j", t=4))
-            sc = work.tile([P, E], U32, name="sc", align_bytes=64)
-            sscale = work.tile([P, E], U8, name="sscale", align_bytes=64)
+        def VIP(b, g, r):
+            if (b, g) not in vi:
+                vi[b, g] = work.tile([P, E, 4], BF16, name="vi", align_bytes=64, bufs=3)
+            nc.scalar.copy(
+                out=vi[b, g][:, 256 * r : 256 * r + 256, :].rearrange("p e j -> p (e j)"), in_=vp[b, g, r][:]
+            )
+
+        def VQ(b, g):
+            vc[b, g] = work.tile([P, E], U32, name="vc%d" % g, align_bytes=64)
+            vs[b, g] = work.tile([P, E], U8, name="vs%d" % g, align_bytes=64)
             nc.vector.quantize_mx(
-                out=sc[:].bitcast(FP8X4), scales=sscale[:], in_=si[:].rearrange("p t m j -> p (t m j)")
+                out=vc[b, g][:].bitcast(FP8X4), scales=vs[b, g][:], in_=vi[b, g][:].rearrange("p e j -> p (e j)")
             )
 
-            qc = work.tile([P, T], U32, name="qc", align_bytes=64)
-            qs = work.tile([P, T], U8, name="qs", align_bytes=64)
-            ysc = work.tile([P, T], U8, name="ysc", align_bytes=64)
-            for h in range(2):
-                qm = work.tile([P, 4, 2, A], BF16, name="qm")
-                nc.vector.tensor_scalar(out=qm[:, :, 0, :], in0=qx[b, h][:], scalar1=0.0, scalar2=None, op0=ALU.is_gt)
-                nc.vector.tensor_scalar(out=qm[:, :, 1, :], in0=qx[b, h][:], scalar1=0.0, scalar2=None, op0=ALU.is_lt)
-                z = work.tile([P, 4, F], BF16, name="z")
-                nc.vector.tensor_tensor(
-                    out=z[:],
-                    in0=qm[:].rearrange("p c h a -> p c (h a)"),
-                    in1=gqb[:].unsqueeze(1).to_broadcast([P, 4, F]),
-                    op=ALU.mult,
+        def KR(b, g):
+            kr[b, g] = work.tile([P, 4, A], BF16, name="kr")
+            for j in range(4):
+                nc.vector.tensor_scalar(
+                    out=kr[b, g][:, j, :],
+                    in0=wk[b, g][:, j, :],
+                    scalar1=ck[b][:, 4 * g + j : 4 * g + j + 1],
+                    scalar2=None,
+                    op0=ALU.mult,
                 )
-                for cc in range(2):
-                    qf = work.tile([P, 2, F], BF16, name="qf")
-                    qt = psum_q.tile([P, 2, 2, P], F32, name="qt")
-                    for ci in range(2):
-                        c = 2 * cc + ci
-                        nc.vector.scalar_tensor_tensor(
-                            out=qf[:, ci, :].rearrange("p (h a) -> p h a", h=2),
-                            in0=uq[h][:, c, :].unsqueeze(1).to_broadcast([P, 2, A]),
-                            scalar=rq[:, 4 * h + c : 4 * h + c + 1],
-                            in1=z[:, c, :].rearrange("p (h a) -> p h a", h=2),
-                            op0=ALU.mult,
-                            op1=ALU.mult,
-                        )
-                        words = qf[:, ci, :].bitcast(F32)
-                        for u in range(2):
-                            nc.tensor.transpose(qt[:, ci, u, :], words[:, u:A:2], ident[:])
-                    qg = work.tile([P, 2, P, 4], BF16, name="qg", align_bytes=64)
-                    nc.scalar.copy(
-                        out=qg[:].rearrange("p c r e -> p (c r e)").bitcast(F32).rearrange("p (c r u) -> p c r u", c=2, u=2),
-                        in_=qt[:].rearrange("p c u r -> p c r u"),
-                    )
-                    tok2 = slice(512 * h + 256 * cc, 512 * h + 256 * cc + 256)
-                    nc.vector.quantize_mx(
-                        out=qc[:, tok2].bitcast(FP8X4), scales=qs[:, tok2], in_=qg[:].rearrange("p c r e -> p (c r e)")
-                    )
-                    yg = work.tile([P, 256, 4], BF16, name="yg", align_bytes=64)
-                    for n in range(2):
-                        r0 = 512 * h + 256 * cc + P * n
-                        tok = slice(r0, r0 + P)
-                        y = psum_o.tile([P, 4, P], F32, name="o")
-                        for t in range(4):
-                            cols = slice(P * t, P * t + P)
-                            nc.tensor.matmul_mx(
-                                out=y[:, t, :],
-                                lhsT=sc[:, cols].bitcast(FP8X4),
-                                lhsT_scale=sscale[:, cols],
-                                rhs=qc[:, tok].bitcast(FP8X4),
-                                rhs_scale=qs[:, tok],
-                                start=True,
-                                stop=True,
-                            )
-                        nc.scalar.activation(
-                            out=yg[:, P * n : P * n + P, :],
-                            in_=y[:].rearrange("p t r -> p r t"),
-                            func=ACT.Copy,
-                            scale=F**-0.5,
-                        )
-                        o = psum_o.tile([P, E], F32, name="o")
-                        nc.tensor.matmul_mx(
-                            out=o[:],
-                            lhsT=qc[:, tok].bitcast(FP8X4),
-                            lhsT_scale=qs[:, tok],
-                            rhs=sc[:].bitcast(FP8X4),
-                            rhs_scale=sscale[:],
-                            start=True,
-                            stop=True,
-                        )
-                        ot = outp.tile([P, E], F32, name="ot")
-                        o_in = o[:].rearrange("p (t m) -> p m t", t=4)
-                        o_out = ot[:].rearrange("p (m t) -> p m t", t=4)
-                        if b == 1 and h == 1:
-                            nc.vector.tensor_scalar(out=o_out, in0=o_in, scalar1=F**-0.5, scalar2=None, op0=ALU.mult)
-                        else:
-                            nc.scalar.activation(out=o_out, in_=o_in, func=ACT.Copy, scale=F**-0.5)
-                        nc.sync.dma_start(out=out_0[b, tok, :], in_=ot[:])
-                    yc = work.tile([P, 256], U32, name="yc", align_bytes=64)
-                    nc.vector.quantize_mx(
-                        out=yc[:].bitcast(FP8X4), scales=ysc[:, tok2], in_=yg[:].rearrange("p r t -> p (r t)")
-                    )
-                    m0 = T * b + 512 * h + 256 * cc
-                    nc.sync.dma_start(
-                        out=out_1[0, :, m0 : m0 + 256, :].rearrange("p m t -> p (m t)").bitcast(I32),
-                        in_=yc[:].bitcast(I32),
-                    )
+
+        def KI(b, g):
+            ki[b, g] = work.tile([P, 4, 64, 4], BF16, name="ki")
+            nc.vector.tensor_copy(out=ki[b, g][:], in_=kr[b, g][:].rearrange("p j (m t) -> p t m j", t=4))
+
+        def KP(b, g):
+            kw[b, g] = work.tile([P, 4, 2, 256], BF16, name="kw", align_bytes=64)
+            nc.vector.tensor_tensor(
+                out=kw[b, g][:, :, 0, :], in0=ki[b, g][:].rearrange("p t m j -> p t (m j)"), in1=mi[b, g][:], op=ALU.mult
+            )
+
+        def KM(b, g):
+            nc.vector.tensor_tensor(
+                out=kw[b, g][:, :, 1, :],
+                in0=ki[b, g][:].rearrange("p t m j -> p t (m j)"),
+                in1=kw[b, g][:, :, 0, :],
+                op=ALU.subtract,
+            )
+
+        def KQ(b, g):
+            kc[b, g] = work.tile([P, F], U32, name="kc%d" % g, align_bytes=64)
+            ks[b, g] = work.tile([P, F], U8, name="ks%d" % g, align_bytes=64)
+            nc.vector.quantize_mx(
+                out=kc[b, g][:].bitcast(FP8X4), scales=ks[b, g][:], in_=kw[b, g][:].rearrange("p t h c -> p (t h c)")
+            )
+
+        def S0(b, t):
+            if b not in s0p:
+                s0p[b] = work.tile([P, 4, E], F32, name="s0p")
+            nc.scalar.activation(out=s0p[b][:, t, :], in_=s0x[b][:, t, :], func=ACT.Copy, scale=gs07[:, t : t + 1])
+
+        def MM(b, t):
+            dd[b, t] = psum_d.tile([P, E], F32, name="d")
+            for g in range(2):
+                cols = slice(P * t, P * t + P)
+                nc.tensor.matmul_mx(
+                    out=dd[b, t][:],
+                    lhsT=kc[b, g][:, cols].bitcast(FP8X4),
+                    lhsT_scale=ks[b, g][:, cols],
+                    rhs=vc[b, g][:].bitcast(FP8X4),
+                    rhs_scale=vs[b, g][:],
+                    start=(g == 0),
+                    stop=(g == 1),
+                )
+
+        def SN(b, t):
+            if b not in sn:
+                sn[b] = work.tile([P, 4, E], BF16, name="sn")
+            nc.vector.scalar_tensor_tensor(
+                out=sn[b][:, t, :],
+                in0=dd[b, t][:],
+                scalar=gs32[:, t : t + 1],
+                in1=s0p[b][:, t, :],
+                op0=ALU.mult,
+                op1=ALU.add,
+            )
+
+        def SI(b, r, eng):
+            if b not in si:
+                si[b] = work.tile([P, 4, P, 4], BF16, name="si", align_bytes=64)
+                sc[b] = work.tile([P, E], U32, name="sc", align_bytes=64)
+                sscale[b] = work.tile([P, E], U8, name="sscale", align_bytes=64)
+            src = sn[b][:].rearrange("p j (m t) -> p t m j", t=4)[:, 2 * r : 2 * r + 2]
+            if eng == "S":
+                nc.scalar.copy(out=si[b][:, 2 * r : 2 * r + 2], in_=src)
+            else:
+                nc.vector.tensor_copy(out=si[b][:, 2 * r : 2 * r + 2], in_=src)
+
+        def SQ(b, r):
+            cols = slice(256 * r, 256 * r + 256)
+            nc.vector.quantize_mx(
+                out=sc[b][:, cols].bitcast(FP8X4),
+                scales=sscale[b][:, cols],
+                in_=si[b][:, 2 * r : 2 * r + 2].rearrange("p t m j -> p (t m j)"),
+            )
+
+        def ZM(b, h):
+            qm[b, h] = work.tile([P, 4, 2, A], BF16, name="qm")
+            nc.vector.tensor_scalar(
+                out=qm[b, h][:, :, 0, :], in0=qx[b, h][:], scalar1=0.0, scalar2=None, op0=ALU.is_gt
+            )
+            nc.vector.tensor_scalar(
+                out=qm[b, h][:, :, 1, :], in0=qx[b, h][:], scalar1=0.0, scalar2=None, op0=ALU.is_lt
+            )
+
+        def Z(b, h):
+            z[b, h] = work.tile([P, 4, F], BF16, name="z")
+            nc.vector.tensor_tensor(
+                out=z[b, h][:],
+                in0=qm[b, h][:].rearrange("p c h a -> p c (h a)"),
+                in1=gqb[:].unsqueeze(1).to_broadcast([P, 4, F]),
+                op=ALU.mult,
+            )
+
+        def QF(b, n):
+            h, c = divmod(n, 4)
+            qf[b, n] = work.tile([P, F], BF16, name="qf", bufs=4)
+            nc.vector.scalar_tensor_tensor(
+                out=qf[b, n][:].rearrange("p (h a) -> p h a", h=2),
+                in0=uq[b, h][:, c, :].unsqueeze(1).to_broadcast([P, 2, A]),
+                scalar=rq[b][:, n : n + 1],
+                in1=z[b, h][:, c, :].rearrange("p (h a) -> p h a", h=2),
+                op0=ALU.mult,
+                op1=ALU.mult,
+            )
+
+        def TR(b, n):
+            if (b, n // 2) not in qt:
+                qt[b, n // 2] = psum_q.tile([P, 2, 2, P], F32, name="qt")
+            words = qf[b, n][:].bitcast(F32)
+            for u in range(2):
+                nc.tensor.transpose(qt[b, n // 2][:, n % 2, u, :], words[:, u:A:2], ident[:])
+
+        def QG(b, cc):
+            qg[b, cc] = work.tile([P, 2, P, 4], BF16, name="qg", align_bytes=64)
+            nc.scalar.copy(
+                out=qg[b, cc][:]
+                .rearrange("p c r e -> p (c r e)")
+                .bitcast(F32)
+                .rearrange("p (c r u) -> p c r u", c=2, u=2),
+                in_=qt[b, cc][:].rearrange("p c u r -> p c r u"),
+            )
+
+        def QQ(b, cc):
+            if b not in qc:
+                qc[b] = work.tile([P, T], U32, name="qc", align_bytes=64)
+                qs[b] = work.tile([P, T], U8, name="qs", align_bytes=64)
+            tok = slice(256 * cc, 256 * cc + 256)
+            nc.vector.quantize_mx(
+                out=qc[b][:, tok].bitcast(FP8X4),
+                scales=qs[b][:, tok],
+                in_=qg[b, cc][:].rearrange("p c r e -> p (c r e)"),
+            )
+
+        def Y(b, n, eng):
+            tok = slice(P * n, P * n + P)
+            if (b, n // 2) not in yg:
+                yg[b, n // 2] = work.tile([P, 256, 4], BF16, name="yg", align_bytes=64, bufs=4)
+            y = psum_o.tile([P, 4, P], F32, name="o")
+            for t in range(4):
+                cols = slice(P * t, P * t + P)
+                nc.tensor.matmul_mx(
+                    out=y[:, t, :],
+                    lhsT=sc[b][:, cols].bitcast(FP8X4),
+                    lhsT_scale=sscale[b][:, cols],
+                    rhs=qc[b][:, tok].bitcast(FP8X4),
+                    rhs_scale=qs[b][:, tok],
+                    start=True,
+                    stop=True,
+                )
+            dst = yg[b, n // 2][:, P * (n % 2) : P * (n % 2) + P, :]
+            src = y[:].rearrange("p t r -> p r t")
+            if eng == "S":
+                nc.scalar.activation(out=dst, in_=src, func=ACT.Copy, scale=F**-0.5)
+            else:
+                nc.vector.tensor_scalar(out=dst, in0=src, scalar1=F**-0.5, scalar2=None, op0=ALU.mult)
+
+        def O(b, n, eng):
+            tok = slice(P * n, P * n + P)
+            o = psum_o.tile([P, E], F32, name="o")
+            nc.tensor.matmul_mx(
+                out=o[:],
+                lhsT=qc[b][:, tok].bitcast(FP8X4),
+                lhsT_scale=qs[b][:, tok],
+                rhs=sc[b][:].bitcast(FP8X4),
+                rhs_scale=sscale[b][:],
+                start=True,
+                stop=True,
+            )
+            ot = outp.tile([P, E], F32, name="ot")
+            src = o[:].rearrange("p (t m) -> p m t", t=4)
+            dst = ot[:].rearrange("p (m t) -> p m t", t=4)
+            if eng == "S":
+                nc.scalar.activation(out=dst, in_=src, func=ACT.Copy, scale=F**-0.5)
+            else:
+                nc.vector.tensor_scalar(out=dst, in0=src, scalar1=F**-0.5, scalar2=None, op0=ALU.mult)
+            nc.sync.dma_start(out=out_0[b, tok, :], in_=ot[:])
+
+        def YQ(b, cc):
+            if b not in ysc:
+                ysc[b] = work.tile([P, T], U8, name="ysc", align_bytes=64)
+            tok = slice(256 * cc, 256 * cc + 256)
+            yc = work.tile([P, 256], U32, name="yc", align_bytes=64, bufs=4)
+            nc.vector.quantize_mx(
+                out=yc[:].bitcast(FP8X4), scales=ysc[b][:, tok], in_=yg[b, cc][:].rearrange("p r t -> p (r t)")
+            )
+            m0 = T * b + 256 * cc
+            nc.sync.dma_start(
+                out=out_1[0, :, m0 : m0 + 256, :].rearrange("p m t -> p (m t)").bitcast(I32), in_=yc[:].bitcast(I32)
+            )
+
+        def YS(b):
             for quad in range(4):
                 nc.sync.dma_start(
                     out=out_2[0, 4 * quad : 4 * quad + 4, T * b : T * b + T].bitcast(I32),
-                    in_=ysc[32 * quad : 32 * quad + 4, :].bitcast(I32),
+                    in_=ysc[b][32 * quad : 32 * quad + 4, :].bitcast(I32),
                 )
+
+        load_k(0, 0)
+        load_small()
+        load_k(0, 1)
+        load_q(0, 0)
+        load_q(0, 1)
+        load_k(1, 0)
+        load_k(1, 1)
+        load_v(0, 0)
+        load_v(0, 1)
+        load_q(1, 0)
+        load_q(1, 1)
+        load_s0(0)
+        load_v(1, 0)
+        load_v(1, 1)
+        load_s0(1)
+        consts()
+        gains()
+        XI(0, 0, "S")
+        VP(0, 1, 0)
+        WK(0, 0)
+        WK(0, 1)
+        ZM(0, 0)
+        WQ(0, 1)
+        XI(0, 1, "S")
+        MI(0, 0)
+        MI(0, 1)
+        WK(1, 0)
+        RK(0, 0)
+        VP(0, 0, 1)
+        RK(0, 1)
+        ZM(0, 1)
+        WK(1, 1)
+        WQ(0, 0)
+        RQ(0, 1)
+        CK(0)
+        VIP(0, 1, 0)
+        WQ(1, 1)
+        KR(0, 0)
+        VIP(0, 0, 1)
+        KR(0, 1)
+        RQ(0, 0)
+        VP(0, 1, 1)
+        VIP(0, 1, 1)
+        VP(1, 0, 1)
+        KI(0, 0)
+        Z(0, 1)
+        CQ(0)
+        Z(0, 0)
+        RK(1, 1)
+        VI(1, 1, "V")
+        ZM(1, 0)
+        VP(0, 0, 0)
+        S0(1, 0)
+        KI(0, 1)
+        QF(0, 1)
+        QF(0, 4)
+        TR(0, 4)
+        VQ(0, 1)
+        QF(0, 0)
+        RK(1, 0)
+        XI(1, 0, "S")
+        KP(0, 1)
+        WQ(1, 0)
+        TR(0, 0)
+        KP(0, 0)
+        KM(0, 1)
+        TR(0, 1)
+        S0(0, 0)
+        KM(0, 0)
+        S0(0, 1)
+        QF(0, 5)
+        VIP(0, 0, 0)
+        KQ(0, 1)
+        S0(1, 2)
+        TR(0, 5)
+        MI(1, 0)
+        KQ(0, 0)
+        QG(0, 2)
+        S0(0, 2)
+        VQ(0, 0)
+        MM(0, 2)
+        S0(0, 3)
+        QF(0, 2)
+        QF(0, 3)
+        VIP(1, 0, 1)
+        QQ(0, 2)
+        XI(1, 1, "S")
+        MM(0, 0)
+        VP(1, 0, 0)
+        QG(0, 0)
+        SN(0, 2)
+        TR(0, 3)
+        CK(1)
+        RQ(1, 1)
+        TR(0, 2)
+        KR(1, 0)
+        KR(1, 1)
+        SN(0, 0)
+        ZM(1, 1)
+        QQ(0, 0)
+        MM(0, 3)
+        MM(0, 1)
+        QG(0, 1)
+        VQ(1, 1)
+        KI(1, 1)
+        S0(1, 3)
+        QF(0, 7)
+        TR(0, 7)
+        SN(0, 1)
+        SN(0, 3)
+        VIP(1, 0, 0)
+        KI(1, 0)
+        QQ(0, 1)
+        KP(1, 0)
+        SI(0, 0, "S")
+        QF(0, 6)
+        S0(1, 1)
+        KM(1, 0)
+        SI(0, 1, "S")
+        RQ(1, 0)
+        Z(1, 0)
+        VQ(1, 0)
+        SQ(0, 0)
+        TR(0, 6)
+        MI(1, 1)
+        QG(0, 3)
+        SQ(0, 1)
+        Y(0, 3, "S")
+        Y(0, 2, "S")
+        KP(1, 1)
+        O(0, 3, "S")
+        KQ(1, 0)
+        KM(1, 1)
+        QQ(0, 3)
+        O(0, 6, "S")
+        Y(0, 1, "S")
+        KQ(1, 1)
+        MM(1, 3)
+        Z(1, 1)
+        O(0, 2, "S")
+        SN(1, 3)
+        MM(1, 0)
+        Y(0, 6, "S")
+        CQ(1)
+        QF(1, 1)
+        QF(1, 0)
+        O(0, 0, "S")
+        MM(1, 2)
+        O(0, 7, "S")
+        TR(1, 1)
+        QF(1, 2)
+        SN(1, 2)
+        SN(1, 0)
+        TR(1, 0)
+        QG(1, 0)
+        O(0, 5, "S")
+        QF(1, 4)
+        O(0, 1, "S")
+        QF(1, 5)
+        Y(0, 7, "S")
+        MM(1, 1)
+        SN(1, 1)
+        SI(1, 1, "S")
+        TR(1, 5)
+        Y(0, 0, "S")
+        TR(1, 4)
+        QF(1, 3)
+        QQ(1, 0)
+        TR(1, 2)
+        TR(1, 3)
+        SI(1, 0, "V")
+        SQ(1, 1)
+        QG(1, 2)
+        YQ(0, 1)
+        SQ(1, 0)
+        QF(1, 7)
+        Y(0, 5, "S")
+        QQ(1, 2)
+        O(0, 4, "S")
+        Y(0, 4, "S")
+        Y(1, 1, "V")
+        QF(1, 6)
+        O(1, 5, "S")
+        YQ(0, 0)
+        YQ(0, 3)
+        QG(1, 1)
+        O(1, 1, "V")
+        QQ(1, 1)
+        Y(1, 4, "S")
+        O(1, 0, "V")
+        TR(1, 6)
+        YQ(0, 2)
+        YS(0)
+        Y(1, 5, "S")
+        YQ(1, 2)
+        TR(1, 7)
+        QG(1, 3)
+        O(1, 3, "S")
+        QQ(1, 3)
+        Y(1, 0, "V")
+        O(1, 2, "S")
+        O(1, 4, "S")
+        O(1, 6, "V")
+        Y(1, 7, "V")
+        YQ(1, 0)
+        Y(1, 2, "S")
+        Y(1, 6, "S")
+        O(1, 7, "V")
+        YQ(1, 3)
+        Y(1, 3, "S")
+        YQ(1, 1)
+        YS(1)

@@ -32,28 +32,34 @@ def tile_dpfpfastweightwriteread_x1_kernel(tc, q, k, v, beta, s0, gq, gs, out_0,
         ctx.enter_context(tc.manual_schedule())
 
         kx, qx, vx, s0x = {}, {}, {}, {}
-        wk, uq, ssk, ssq, ck, rq = {}, {}, {}, {}, {}, {}
-        xi, mi, vi, kr, ki, kw, kc, ks, vc, vs = {}, {}, {}, {}, {}, {}, {}, {}, {}, {}
-        vp = {}
+        wk, uq, ss, r, ck = {}, {}, {}, {}, {}
+        mi, xp, vi, vp, kr, ki, kw, kc, ks, vc, vs = {}, {}, {}, {}, {}, {}, {}, {}, {}, {}, {}
         s0p, sn, si, sc, sscale = {}, {}, {}, {}, {}
         qm, z, qf, qt, qg, qc, qs, yg, ysc, dd = {}, {}, {}, {}, {}, {}, {}, {}, {}, {}
 
-        beta_sb = keep.tile([P, B * 2 * 4], BF16, name="beta_sb")
-        gs_sb = keep.tile([P, 4], BF16, name="gs_sb")
+        rows = keep.tile([P, F], BF16, name="rows")
+        csm = keep.tile([P, 4, 8], BF16, name="csm")
         gqb = keep.tile([P, F], BF16, name="gqb")
-        neg_half = keep.tile([P, 8], F32, name="neg_half")
         ident = keep.tile([P, P], F32, name="ident")
         ident16 = keep.tile([P, P], BF16, name="ident16")
         gs07 = keep.tile([P, 4], F32, name="gs07")
         gs32 = keep.tile([P, 4], F32, name="gs32")
 
         def load_k(b, g):
-            kx[b, g] = keep.tile([P, 4, A], BF16, name="kx%d%d" % (b, g))
-            nc.sync.dma_start(out=kx[b, g][:], in_=k[b, 512 * g : 512 * g + 512, :].rearrange("(p j) a -> p j a", j=4))
+            if b not in kx:
+                kx[b] = keep.tile([P, 8, A], BF16, name="kx%d" % b)
+            nc.sync.dma_start(
+                out=kx[b][:, 4 * g : 4 * g + 4, :],
+                in_=k[b, 512 * g : 512 * g + 512, :].rearrange("(p j) a -> p j a", j=4),
+            )
 
         def load_q(b, h):
-            qx[b, h] = keep.tile([P, 4, A], BF16, name="qx%d%d" % (b, h))
-            nc.sync.dma_start(out=qx[b, h][:], in_=q[b, 512 * h : 512 * h + 512, :].rearrange("(c p) a -> p c a", p=P))
+            if b not in qx:
+                qx[b] = keep.tile([P, 8, A], BF16, name="qx%d" % b)
+            nc.sync.dma_start(
+                out=qx[b][:, 4 * h : 4 * h + 4, :],
+                in_=q[b, 512 * h : 512 * h + 512, :].rearrange("(c p) a -> p c a", p=P),
+            )
 
         def load_v(b, g):
             vx[b, g] = keep.tile([P, 4, E], BF16, name="vx%d%d" % (b, g))
@@ -63,24 +69,31 @@ def tile_dpfpfastweightwriteread_x1_kernel(tc, q, k, v, beta, s0, gq, gs, out_0,
             s0x[b] = keep.tile([P, 4, E], BF16, name="s0x%d" % b)
             nc.sync.dma_start(out=s0x[b][:], in_=s0[b].rearrange("(p j) e -> p j e", j=4))
 
-        def load_small():
-            nc.scalar.dma_start(
-                out=beta_sb[:].rearrange("p (r j) -> p r j", j=4),
-                in_=beta.rearrange("b (g p j) -> p (b g) j", g=2, j=4),
-            )
-            nc.scalar.dma_start(out=gs_sb[:], in_=gs.rearrange("(p j) -> p j", j=4))
-            nc.scalar.dma_start(out=gqb[:], in_=gq.partition_broadcast(P))
-
         def consts():
-            nc.gpsimd.memset(neg_half[:], -0.5)
-            make_identity(nc, ident[:])
+            nc.gpsimd.memset(rows[:], 0.0)
             make_identity(nc, ident16[:])
+            make_identity(nc, ident[:])
+
+        def load_small():
+            nc.scalar.dma_start(out=rows[0:4, :], in_=beta.rearrange("b (g x) -> (b g) x", g=2))
+            nc.scalar.dma_start(out=rows[4:5, :], in_=gs.rearrange("(o x) -> o x", o=1))
+            nc.scalar.dma_start(out=rows[5:6, :], in_=gq.rearrange("(o x) -> o x", o=1))
+
+        def GA():
+            t = psum_o.tile([P, 4, P], BF16, name="o")
+            for j in range(4):
+                nc.tensor.transpose(t[:, j, :], rows[:, j:F:4], ident16[:])
+            nc.scalar.copy(out=csm[:], in_=t[:, :, 0:8])
+
+        def GB():
+            t = psum_o.tile([P, 4, P], BF16, name="o")
+            for j in range(4):
+                nc.tensor.transpose(t[:, j, :], csm[:, j, 5:6].to_broadcast([P, P]), ident16[:])
+            nc.scalar.copy(out=gqb[:].rearrange("p (n j) -> p n j", j=4), in_=t[:].rearrange("p j n -> p n j"))
 
         def gains():
-            nc.gpsimd.tensor_scalar(out=gs07[:], in0=gs_sb[:], scalar1=0.7, scalar2=0.0, op0=ALU.mult, op1=ALU.add)
-            nc.gpsimd.tensor_scalar(
-                out=gs32[:], in0=gs_sb[:], scalar1=1.0 / 32.0, scalar2=0.0, op0=ALU.mult, op1=ALU.add
-            )
+            nc.scalar.mul(gs07[:], csm[:, :, 4], 0.7)
+            nc.scalar.mul(gs32[:], csm[:, :, 4], 1.0 / 32.0)
 
         def products(x, w):
             nc.vector.tensor_tensor(out=w[:, :, 1:A], in0=x[:, :, 1:A], in1=x[:, :, 0 : A - 1], op=ALU.mult)
@@ -88,91 +101,96 @@ def tile_dpfpfastweightwriteread_x1_kernel(tc, q, k, v, beta, s0, gq, gs, out_0,
                 out=w[:, :, 0:1], in0=x[:, :, 0:1], scalar=-1.0, in1=x[:, :, A - 1 : A], op0=ALU.mult, op1=ALU.mult
             )
 
-        def squares(w, ss, base):
-            nc.scalar.activation(out=w[:], in_=w[:], func=ACT.Relu)
+        def squares(w, b, base):
+            nc.scalar.activation(out=w, in_=w, func=ACT.Relu)
+            if b not in ss:
+                ss[b] = small.tile([P, 16], F32, name="ss")
             for j in range(4):
                 junk = small.tile([P, A], BF16, name="junk")
                 nc.scalar.activation(
-                    out=junk[:], in_=w[:, j, :], func=ACT.Square, accum_out=ss[:, base + j : base + j + 1]
+                    out=junk[:], in_=w[:, j, :], func=ACT.Square, accum_out=ss[b][:, base + j : base + j + 1]
                 )
 
-        def inv_rms(ss, r):
-            ms = small.tile([P, 8], F32, name="ms")
-            nc.gpsimd.tensor_scalar(out=ms[:], in0=ss[:], scalar1=1.0 / F, scalar2=1e-6, op0=ALU.mult, op1=ALU.add)
-            nc.gpsimd.tensor_tensor(out=r[:], in0=ms[:], in1=neg_half[:], op=ALU.pow)
+        def WK(b, g=None):
+            if b not in wk:
+                wk[b] = work.tile([P, 8, A], F32, name="wk")
+            part = slice(0, 8) if g is None else slice(4 * g, 4 * g + 4)
+            products(kx[b][:, part, :], wk[b][:, part, :])
 
-        def WK(b, g):
-            wk[b, g] = work.tile([P, 4, A], F32, name="wk%d" % g)
-            products(kx[b, g], wk[b, g])
+        def WQ(b):
+            uq[b] = work.tile([P, 8, A], F32, name="uq")
+            products(qx[b][:], uq[b][:])
 
         def RK(b, g):
-            if b not in ssk:
-                ssk[b] = small.tile([P, 8], F32, name="ssk")
-            squares(wk[b, g], ssk[b], 4 * g)
-
-        def CK(b):
-            rk = small.tile([P, 8], F32, name="rk")
-            inv_rms(ssk[b], rk)
-            ck[b] = small.tile([P, 8], F32, name="ck")
-            nc.gpsimd.tensor_tensor(out=ck[b][:], in0=rk[:], in1=beta_sb[:, 8 * b : 8 * b + 8], op=ALU.mult)
-
-        def WQ(b, h):
-            uq[b, h] = work.tile([P, 4, A], F32, name="uq%d" % h)
-            products(qx[b, h], uq[b, h])
+            squares(wk[b][:, 4 * g : 4 * g + 4, :], b, 4 * g)
 
         def RQ(b, h):
-            if b not in ssq:
-                ssq[b] = small.tile([P, 8], F32, name="ssq")
-            squares(uq[b, h], ssq[b], 4 * h)
+            squares(uq[b][:, 4 * h : 4 * h + 4, :], b, 8 + 4 * h)
 
-        def CQ(b):
-            rq[b] = small.tile([P, 8], F32, name="rq")
-            inv_rms(ssq[b], rq[b])
-
-        def XI(b, g, eng):
-            xi[b, g] = work.tile([P, 4, 64, 4], BF16, name="xi")
-            src = kx[b, g][:].rearrange("p j (m t) -> p t m j", t=4)
-            if eng == "S":
-                nc.scalar.copy(out=xi[b, g][:], in_=src)
+        def CH(b, i):
+            if i == 0:
+                r[b] = small.tile([P, 16], F32, name="r")
+                nc.vector.tensor_scalar(
+                    out=ss[b][:], in0=ss[b][:], scalar1=1.0 / F, scalar2=1e-6, op0=ALU.mult, op1=ALU.add
+                )
+            elif i == 1:
+                nc.scalar.activation(out=r[b][:], in_=ss[b][:], func=ACT.Sqrt)
+            elif i == 2:
+                nc.vector.reciprocal(out=r[b][:], in_=r[b][:])
             else:
-                nc.vector.tensor_copy(out=xi[b, g][:], in_=src)
+                ck[b] = small.tile([P, 8], F32, name="ck")
+                nc.vector.tensor_tensor(
+                    out=ck[b][:].rearrange("p (g j) -> p g j", g=2),
+                    in0=r[b][:, 0:8].rearrange("p (g j) -> p g j", g=2),
+                    in1=csm[:, :, 2 * b : 2 * b + 2].rearrange("p j g -> p g j"),
+                    op=ALU.mult,
+                )
 
-        def MI(b, g):
-            mi[b, g] = work.tile([P, 4, 256], BF16, name="mi")
-            nc.vector.tensor_scalar(
-                out=mi[b, g][:],
-                in0=xi[b, g][:].rearrange("p t m j -> p t (m j)"),
-                scalar1=0.0,
-                scalar2=None,
-                op0=ALU.is_gt,
-            )
+        def MI(b):
+            mi[b] = work.tile([P, 8, A], BF16, name="mi")
+            nc.vector.tensor_scalar(out=mi[b][:], in0=kx[b][:], scalar1=0.0, scalar2=None, op0=ALU.is_gt)
 
-        def VI(b, g, eng):
-            vi[b, g] = work.tile([P, E, 4], BF16, name="vi", align_bytes=64, bufs=3)
-            if eng == "S":
-                nc.scalar.copy(out=vi[b, g][:], in_=vx[b, g][:].rearrange("p j e -> p e j"))
-            else:
-                nc.vector.tensor_copy(out=vi[b, g][:], in_=vx[b, g][:].rearrange("p j e -> p e j"))
+        def XP(b, g):
+            xp[b, g] = psum_d.tile([P, 4, 256], BF16, name="d")
+            src = mi[b][:, 4 * g : 4 * g + 4, :].rearrange("p j (m t) -> p t m j", t=4)
+            for i in range(2):
+                nc.tensor.matmul(
+                    out=xp[b, g][:, 2 * i : 2 * i + 2, :].rearrange("p t c -> p (t c)"),
+                    lhsT=ident16[:],
+                    rhs=src[:, 2 * i : 2 * i + 2],
+                    start=True,
+                    stop=True,
+                )
 
-        def VP(b, g, r):
-            vp[b, g, r] = psum_o.tile([P, 2 * E], BF16, name="o")
+        def VP(b, g, h):
+            vp[b, g, h] = psum_o.tile([P, 2 * E], BF16, name="o")
             src = vx[b, g][:].rearrange("p j e -> p e j")
             for i in range(2):
-                e0 = 256 * r + 128 * i
+                e0 = 256 * h + 128 * i
                 nc.tensor.matmul(
-                    out=vp[b, g, r][:, E * i : E * i + E],
+                    out=vp[b, g, h][:, E * i : E * i + E],
                     lhsT=ident16[:],
                     rhs=src[:, e0 : e0 + 128, :],
                     start=True,
                     stop=True,
                 )
 
-        def VIP(b, g, r):
+        def new_vi(b, g):
             if (b, g) not in vi:
                 vi[b, g] = work.tile([P, E, 4], BF16, name="vi", align_bytes=64, bufs=3)
+
+        def VIP(b, g, h):
+            new_vi(b, g)
             nc.scalar.copy(
-                out=vi[b, g][:, 256 * r : 256 * r + 256, :].rearrange("p e j -> p (e j)"), in_=vp[b, g, r][:]
+                out=vi[b, g][:, 256 * h : 256 * h + 256, :].rearrange("p e j -> p (e j)"), in_=vp[b, g, h][:]
             )
+
+        def VI(b, g, eng):
+            new_vi(b, g)
+            if eng == "S":
+                nc.scalar.copy(out=vi[b, g][:], in_=vx[b, g][:].rearrange("p j e -> p e j"))
+            else:
+                nc.vector.tensor_copy(out=vi[b, g][:], in_=vx[b, g][:].rearrange("p j e -> p e j"))
 
         def VQ(b, g):
             vc[b, g] = work.tile([P, E], U32, name="vc%d" % g, align_bytes=64)
@@ -181,33 +199,37 @@ def tile_dpfpfastweightwriteread_x1_kernel(tc, q, k, v, beta, s0, gq, gs, out_0,
                 out=vc[b, g][:].bitcast(FP8X4), scales=vs[b, g][:], in_=vi[b, g][:].rearrange("p e j -> p (e j)")
             )
 
-        def KR(b, g):
+        def KR(b, g, eng):
             kr[b, g] = work.tile([P, 4, A], BF16, name="kr")
             for j in range(4):
-                nc.vector.tensor_scalar(
-                    out=kr[b, g][:, j, :],
-                    in0=wk[b, g][:, j, :],
-                    scalar1=ck[b][:, 4 * g + j : 4 * g + j + 1],
-                    scalar2=None,
-                    op0=ALU.mult,
-                )
+                n = 4 * g + j
+                if eng == "S":
+                    nc.scalar.activation(
+                        out=kr[b, g][:, j, :], in_=wk[b][:, n, :], func=ACT.Copy, scale=ck[b][:, n : n + 1]
+                    )
+                else:
+                    nc.vector.tensor_scalar(
+                        out=kr[b, g][:, j, :],
+                        in0=wk[b][:, n, :],
+                        scalar1=ck[b][:, n : n + 1],
+                        scalar2=None,
+                        op0=ALU.mult,
+                    )
 
         def KI(b, g):
-            ki[b, g] = work.tile([P, 4, 64, 4], BF16, name="ki")
-            nc.vector.tensor_copy(out=ki[b, g][:], in_=kr[b, g][:].rearrange("p j (m t) -> p t m j", t=4))
+            ki[b, g] = work.tile([P, 4, 256], BF16, name="ki")
+            nc.vector.tensor_copy(
+                out=ki[b, g][:].rearrange("p t (m c) -> p m t c", c=8),
+                in_=kr[b, g][:].rearrange("p j (m i t) -> p m t i j", i=2, t=4),
+            )
 
         def KP(b, g):
             kw[b, g] = work.tile([P, 4, 2, 256], BF16, name="kw", align_bytes=64)
-            nc.vector.tensor_tensor(
-                out=kw[b, g][:, :, 0, :], in0=ki[b, g][:].rearrange("p t m j -> p t (m j)"), in1=mi[b, g][:], op=ALU.mult
-            )
+            nc.vector.tensor_tensor(out=kw[b, g][:, :, 0, :], in0=ki[b, g][:], in1=xp[b, g][:], op=ALU.mult)
 
         def KM(b, g):
             nc.vector.tensor_tensor(
-                out=kw[b, g][:, :, 1, :],
-                in0=ki[b, g][:].rearrange("p t m j -> p t (m j)"),
-                in1=kw[b, g][:, :, 0, :],
-                op=ALU.subtract,
+                out=kw[b, g][:, :, 1, :], in0=ki[b, g][:], in1=kw[b, g][:, :, 0, :], op=ALU.subtract
             )
 
         def KQ(b, g):
@@ -248,33 +270,26 @@ def tile_dpfpfastweightwriteread_x1_kernel(tc, q, k, v, beta, s0, gq, gs, out_0,
                 op1=ALU.add,
             )
 
-        def SI(b, r, eng):
+        def SI(b, h):
             if b not in si:
-                si[b] = work.tile([P, 4, P, 4], BF16, name="si", align_bytes=64)
-                sc[b] = work.tile([P, E], U32, name="sc", align_bytes=64)
-                sscale[b] = work.tile([P, E], U8, name="sscale", align_bytes=64)
-            src = sn[b][:].rearrange("p j (m t) -> p t m j", t=4)[:, 2 * r : 2 * r + 2]
-            if eng == "S":
-                nc.scalar.copy(out=si[b][:, 2 * r : 2 * r + 2], in_=src)
-            else:
-                nc.vector.tensor_copy(out=si[b][:, 2 * r : 2 * r + 2], in_=src)
+                si[b] = work.tile([P, 4, P * 4], BF16, name="si", align_bytes=64)
+            nc.vector.tensor_copy(
+                out=si[b][:].rearrange("p t (m c) -> p m t c", c=8)[:, 32 * h : 32 * h + 32],
+                in_=sn[b][:].rearrange("p j (m i t) -> p m t i j", i=2, t=4)[:, 32 * h : 32 * h + 32],
+            )
 
-        def SQ(b, r):
-            cols = slice(256 * r, 256 * r + 256)
+        def SQ(b):
+            sc[b] = work.tile([P, E], U32, name="sc", align_bytes=64)
+            sscale[b] = work.tile([P, E], U8, name="sscale", align_bytes=64)
             nc.vector.quantize_mx(
-                out=sc[b][:, cols].bitcast(FP8X4),
-                scales=sscale[b][:, cols],
-                in_=si[b][:, 2 * r : 2 * r + 2].rearrange("p t m j -> p (t m j)"),
+                out=sc[b][:].bitcast(FP8X4), scales=sscale[b][:], in_=si[b][:].rearrange("p t c -> p (t c)")
             )
 
         def ZM(b, h):
             qm[b, h] = work.tile([P, 4, 2, A], BF16, name="qm")
-            nc.vector.tensor_scalar(
-                out=qm[b, h][:, :, 0, :], in0=qx[b, h][:], scalar1=0.0, scalar2=None, op0=ALU.is_gt
-            )
-            nc.vector.tensor_scalar(
-                out=qm[b, h][:, :, 1, :], in0=qx[b, h][:], scalar1=0.0, scalar2=None, op0=ALU.is_lt
-            )
+            src = qx[b][:, 4 * h : 4 * h + 4, :]
+            nc.vector.tensor_scalar(out=qm[b, h][:, :, 0, :], in0=src, scalar1=0.0, scalar2=None, op0=ALU.is_gt)
+            nc.vector.tensor_scalar(out=qm[b, h][:, :, 1, :], in0=src, scalar1=0.0, scalar2=None, op0=ALU.is_lt)
 
         def Z(b, h):
             z[b, h] = work.tile([P, 4, F], BF16, name="z")
@@ -286,13 +301,12 @@ def tile_dpfpfastweightwriteread_x1_kernel(tc, q, k, v, beta, s0, gq, gs, out_0,
             )
 
         def QF(b, n):
-            h, c = divmod(n, 4)
             qf[b, n] = work.tile([P, F], BF16, name="qf", bufs=4)
             nc.vector.scalar_tensor_tensor(
                 out=qf[b, n][:].rearrange("p (h a) -> p h a", h=2),
-                in0=uq[b, h][:, c, :].unsqueeze(1).to_broadcast([P, 2, A]),
-                scalar=rq[b][:, n : n + 1],
-                in1=z[b, h][:, c, :].rearrange("p (h a) -> p h a", h=2),
+                in0=uq[b][:, n, :].unsqueeze(1).to_broadcast([P, 2, A]),
+                scalar=r[b][:, 8 + n : 9 + n],
+                in1=z[b, n // 4][:, n % 4, :].rearrange("p (h a) -> p h a", h=2),
                 op0=ALU.mult,
                 op1=ALU.mult,
             )
@@ -304,26 +318,32 @@ def tile_dpfpfastweightwriteread_x1_kernel(tc, q, k, v, beta, s0, gq, gs, out_0,
             for u in range(2):
                 nc.tensor.transpose(qt[b, n // 2][:, n % 2, u, :], words[:, u:A:2], ident[:])
 
-        def QG(b, cc):
-            qg[b, cc] = work.tile([P, 2, P, 4], BF16, name="qg", align_bytes=64)
+        def QG(b, c):
+            qg[b, c] = work.tile([P, 2, P, 4], BF16, name="qg", align_bytes=64)
             nc.scalar.copy(
-                out=qg[b, cc][:]
+                out=qg[b, c][:]
                 .rearrange("p c r e -> p (c r e)")
                 .bitcast(F32)
                 .rearrange("p (c r u) -> p c r u", c=2, u=2),
-                in_=qt[b, cc][:].rearrange("p c u r -> p c r u"),
+                in_=qt[b, c][:].rearrange("p c u r -> p c r u"),
             )
 
-        def QQ(b, cc):
+        def QQ(b, c):
             if b not in qc:
                 qc[b] = work.tile([P, T], U32, name="qc", align_bytes=64)
                 qs[b] = work.tile([P, T], U8, name="qs", align_bytes=64)
-            tok = slice(256 * cc, 256 * cc + 256)
+            tok = slice(256 * c, 256 * c + 256)
             nc.vector.quantize_mx(
                 out=qc[b][:, tok].bitcast(FP8X4),
                 scales=qs[b][:, tok],
-                in_=qg[b, cc][:].rearrange("p c r e -> p (c r e)"),
+                in_=qg[b, c][:].rearrange("p c r e -> p (c r e)"),
             )
+
+        def scaled(eng, dst, src):
+            if eng == "S":
+                nc.scalar.activation(out=dst, in_=src, func=ACT.Copy, scale=F**-0.5)
+            else:
+                nc.vector.tensor_scalar(out=dst, in0=src, scalar1=F**-0.5, scalar2=None, op0=ALU.mult)
 
         def Y(b, n, eng):
             tok = slice(P * n, P * n + P)
@@ -341,12 +361,7 @@ def tile_dpfpfastweightwriteread_x1_kernel(tc, q, k, v, beta, s0, gq, gs, out_0,
                     start=True,
                     stop=True,
                 )
-            dst = yg[b, n // 2][:, P * (n % 2) : P * (n % 2) + P, :]
-            src = y[:].rearrange("p t r -> p r t")
-            if eng == "S":
-                nc.scalar.activation(out=dst, in_=src, func=ACT.Copy, scale=F**-0.5)
-            else:
-                nc.vector.tensor_scalar(out=dst, in0=src, scalar1=F**-0.5, scalar2=None, op0=ALU.mult)
+            scaled(eng, yg[b, n // 2][:, P * (n % 2) : P * (n % 2) + P, :], y[:].rearrange("p t r -> p r t"))
 
         def O(b, n, eng):
             tok = slice(P * n, P * n + P)
@@ -361,23 +376,18 @@ def tile_dpfpfastweightwriteread_x1_kernel(tc, q, k, v, beta, s0, gq, gs, out_0,
                 stop=True,
             )
             ot = outp.tile([P, E], F32, name="ot")
-            src = o[:].rearrange("p (t m) -> p m t", t=4)
-            dst = ot[:].rearrange("p (m t) -> p m t", t=4)
-            if eng == "S":
-                nc.scalar.activation(out=dst, in_=src, func=ACT.Copy, scale=F**-0.5)
-            else:
-                nc.vector.tensor_scalar(out=dst, in0=src, scalar1=F**-0.5, scalar2=None, op0=ALU.mult)
+            scaled(eng, ot[:].rearrange("p (m t) -> p m t", t=4), o[:].rearrange("p (t m) -> p m t", t=4))
             nc.sync.dma_start(out=out_0[b, tok, :], in_=ot[:])
 
-        def YQ(b, cc):
+        def YQ(b, c):
             if b not in ysc:
                 ysc[b] = work.tile([P, T], U8, name="ysc", align_bytes=64)
-            tok = slice(256 * cc, 256 * cc + 256)
+            tok = slice(256 * c, 256 * c + 256)
             yc = work.tile([P, 256], U32, name="yc", align_bytes=64, bufs=4)
             nc.vector.quantize_mx(
-                out=yc[:].bitcast(FP8X4), scales=ysc[b][:, tok], in_=yg[b, cc][:].rearrange("p r t -> p (r t)")
+                out=yc[:].bitcast(FP8X4), scales=ysc[b][:, tok], in_=yg[b, c][:].rearrange("p r t -> p (r t)")
             )
-            m0 = T * b + 256 * cc
+            m0 = T * b + 256 * c
             nc.sync.dma_start(
                 out=out_1[0, :, m0 : m0 + 256, :].rearrange("p m t -> p (m t)").bitcast(I32), in_=yc[:].bitcast(I32)
             )
@@ -389,6 +399,7 @@ def tile_dpfpfastweightwriteread_x1_kernel(tc, q, k, v, beta, s0, gq, gs, out_0,
                     in_=ysc[b][32 * quad : 32 * quad + 4, :].bitcast(I32),
                 )
 
+        consts()
         load_k(0, 0)
         load_small()
         load_k(0, 1)
@@ -404,200 +415,192 @@ def tile_dpfpfastweightwriteread_x1_kernel(tc, q, k, v, beta, s0, gq, gs, out_0,
         load_v(1, 0)
         load_v(1, 1)
         load_s0(1)
-        consts()
-        gains()
-        XI(0, 0, "S")
-        VP(0, 1, 0)
-        WK(0, 0)
-        WK(0, 1)
-        ZM(0, 0)
-        WQ(0, 1)
-        XI(0, 1, "S")
-        MI(0, 0)
-        MI(0, 1)
-        WK(1, 0)
-        RK(0, 0)
         VP(0, 0, 1)
+        WK(0, 0)
+        RK(0, 0)
+        MI(0)
+        WK(0, 1)
         RK(0, 1)
         ZM(0, 1)
-        WK(1, 1)
-        WQ(0, 0)
-        RQ(0, 1)
-        CK(0)
-        VIP(0, 1, 0)
-        WQ(1, 1)
-        KR(0, 0)
+        WQ(0)
+        WK(1)
+        GA()
+        gains()
         VIP(0, 0, 1)
-        KR(0, 1)
-        RQ(0, 0)
-        VP(0, 1, 1)
-        VIP(0, 1, 1)
-        VP(1, 0, 1)
-        KI(0, 0)
-        Z(0, 1)
-        CQ(0)
+        RQ(0, 1)
+        ZM(0, 0)
+        XP(0, 0)
+        WQ(1)
+        GB()
         Z(0, 0)
-        RK(1, 1)
-        VI(1, 1, "V")
-        ZM(1, 0)
+        RQ(0, 0)
+        MI(1)
+        CH(0, 0)
+        Z(0, 1)
         VP(0, 0, 0)
-        S0(1, 0)
-        KI(0, 1)
+        VIP(0, 0, 0)
+        CH(0, 1)
+        CH(0, 2)
+        VQ(0, 0)
+        VI(0, 1, "S")
+        QF(0, 2)
+        CH(0, 3)
+        QF(0, 3)
+        KR(0, 0, "S")
+        VI(1, 0, "V")
         QF(0, 1)
+        KI(0, 0)
+        QF(0, 0)
+        TR(0, 2)
+        TR(0, 3)
+        QG(0, 1)
+        XP(0, 1)
+        ZM(1, 1)
+        KR(0, 1, "S")
+        KI(0, 1)
+        S0(0, 3)
+        RQ(1, 0)
+        RK(1, 0)
+        KP(0, 0)
+        KP(0, 1)
+        S0(0, 0)
+        S0(0, 1)
+        TR(0, 0)
+        QQ(0, 1)
+        KM(0, 1)
+        KM(0, 0)
+        KQ(0, 1)
+        KQ(0, 0)
+        TR(0, 1)
+        QG(0, 0)
         QF(0, 4)
         TR(0, 4)
         VQ(0, 1)
-        QF(0, 0)
-        RK(1, 0)
-        XI(1, 0, "S")
-        KP(0, 1)
-        WQ(1, 0)
-        TR(0, 0)
-        KP(0, 0)
-        KM(0, 1)
-        TR(0, 1)
-        S0(0, 0)
-        KM(0, 0)
-        S0(0, 1)
-        QF(0, 5)
-        VIP(0, 0, 0)
-        KQ(0, 1)
-        S0(1, 2)
-        TR(0, 5)
-        MI(1, 0)
-        KQ(0, 0)
-        QG(0, 2)
-        S0(0, 2)
-        VQ(0, 0)
-        MM(0, 2)
-        S0(0, 3)
-        QF(0, 2)
-        QF(0, 3)
-        VIP(1, 0, 1)
-        QQ(0, 2)
-        XI(1, 1, "S")
-        MM(0, 0)
-        VP(1, 0, 0)
-        QG(0, 0)
-        SN(0, 2)
-        TR(0, 3)
-        CK(1)
-        RQ(1, 1)
-        TR(0, 2)
-        KR(1, 0)
-        KR(1, 1)
-        SN(0, 0)
-        ZM(1, 1)
-        QQ(0, 0)
-        MM(0, 3)
         MM(0, 1)
-        QG(0, 1)
-        VQ(1, 1)
-        KI(1, 1)
-        S0(1, 3)
         QF(0, 7)
-        TR(0, 7)
+        MM(0, 2)
+        QF(0, 5)
+        ZM(1, 0)
+        TR(0, 5)
+        S0(0, 2)
         SN(0, 1)
-        SN(0, 3)
-        VIP(1, 0, 0)
-        KI(1, 0)
-        QQ(0, 1)
-        KP(1, 0)
-        SI(0, 0, "S")
-        QF(0, 6)
-        S0(1, 1)
-        KM(1, 0)
-        SI(0, 1, "S")
-        RQ(1, 0)
-        Z(1, 0)
         VQ(1, 0)
-        SQ(0, 0)
+        SN(0, 2)
+        RQ(1, 1)
+        RK(1, 1)
+        MM(0, 0)
+        MM(0, 3)
+        Z(1, 1)
+        QF(0, 6)
         TR(0, 6)
-        MI(1, 1)
+        SN(0, 0)
+        TR(0, 7)
+        XP(1, 1)
+        Z(1, 0)
+        QQ(0, 0)
+        CH(1, 0)
+        SN(0, 3)
+        QG(0, 2)
+        QQ(0, 2)
+        CH(1, 1)
+        CH(1, 2)
         QG(0, 3)
-        SQ(0, 1)
-        Y(0, 3, "S")
-        Y(0, 2, "S")
-        KP(1, 1)
-        O(0, 3, "S")
-        KQ(1, 0)
-        KM(1, 1)
+        XP(1, 0)
+        SI(0, 0)
+        QF(1, 0)
+        VI(1, 1, "S")
+        TR(1, 0)
+        CH(1, 3)
+        KR(1, 1, "S")
+        SI(0, 1)
+        QF(1, 3)
+        TR(1, 3)
+        SQ(0)
         QQ(0, 3)
-        O(0, 6, "S")
+        QF(1, 1)
+        KI(1, 1)
+        KR(1, 0, "S")
+        Y(0, 0, "S")
+        VQ(1, 1)
+        KI(1, 0)
+        Y(0, 7, "S")
+        Y(0, 4, "S")
+        QF(1, 2)
+        S0(1, 1)
+        O(0, 5, "S")
+        S0(1, 2)
+        KP(1, 1)
+        KP(1, 0)
+        Y(0, 5, "S")
+        KM(1, 1)
+        Y(0, 6, "S")
+        KM(1, 0)
+        Y(0, 3, "S")
+        TR(1, 2)
+        TR(1, 1)
         Y(0, 1, "S")
         KQ(1, 1)
-        MM(1, 3)
-        Z(1, 1)
-        O(0, 2, "S")
-        SN(1, 3)
-        MM(1, 0)
-        Y(0, 6, "S")
-        CQ(1)
-        QF(1, 1)
-        QF(1, 0)
-        O(0, 0, "S")
-        MM(1, 2)
-        O(0, 7, "S")
-        TR(1, 1)
-        QF(1, 2)
-        SN(1, 2)
-        SN(1, 0)
-        TR(1, 0)
-        QG(1, 0)
-        O(0, 5, "S")
-        QF(1, 4)
+        KQ(1, 0)
+        S0(1, 3)
+        YQ(0, 3)
         O(0, 1, "S")
+        S0(1, 0)
+        QG(1, 1)
+        Y(0, 2, "S")
+        MM(1, 2)
+        QG(1, 0)
+        QF(1, 7)
+        QF(1, 4)
+        O(0, 0, "S")
+        O(0, 4, "S")
+        YQ(0, 2)
+        SN(1, 2)
         QF(1, 5)
-        Y(0, 7, "S")
+        MM(1, 0)
+        SN(1, 0)
         MM(1, 1)
         SN(1, 1)
-        SI(1, 1, "S")
-        TR(1, 5)
-        Y(0, 0, "S")
-        TR(1, 4)
-        QF(1, 3)
-        QQ(1, 0)
-        TR(1, 2)
-        TR(1, 3)
-        SI(1, 0, "V")
-        SQ(1, 1)
-        QG(1, 2)
-        YQ(0, 1)
-        SQ(1, 0)
-        QF(1, 7)
-        Y(0, 5, "S")
-        QQ(1, 2)
-        O(0, 4, "S")
-        Y(0, 4, "S")
-        Y(1, 1, "V")
         QF(1, 6)
-        O(1, 5, "S")
-        YQ(0, 0)
-        YQ(0, 3)
-        QG(1, 1)
-        O(1, 1, "V")
+        MM(1, 3)
+        SN(1, 3)
         QQ(1, 1)
-        Y(1, 4, "S")
-        O(1, 0, "V")
+        SI(1, 0)
+        SI(1, 1)
+        O(0, 7, "S")
+        O(0, 2, "S")
+        YQ(0, 1)
+        SQ(1)
+        TR(1, 4)
+        TR(1, 5)
         TR(1, 6)
-        YQ(0, 2)
-        YS(0)
-        Y(1, 5, "S")
-        YQ(1, 2)
+        QG(1, 2)
+        QQ(1, 0)
+        QQ(1, 2)
         TR(1, 7)
+        O(0, 3, "S")
+        O(0, 6, "S")
+        YQ(0, 0)
+        YS(0)
+        O(1, 1, "V")
         QG(1, 3)
-        O(1, 3, "S")
+        Y(1, 2, "S")
+        O(1, 5, "V")
+        O(1, 0, "S")
+        O(1, 2, "S")
         QQ(1, 3)
         Y(1, 0, "V")
-        O(1, 2, "S")
-        O(1, 4, "S")
-        O(1, 6, "V")
-        Y(1, 7, "V")
-        YQ(1, 0)
-        Y(1, 2, "S")
-        Y(1, 6, "S")
-        O(1, 7, "V")
-        YQ(1, 3)
         Y(1, 3, "S")
+        O(1, 3, "V")
+        O(1, 6, "S")
         YQ(1, 1)
+        Y(1, 5, "S")
+        Y(1, 4, "V")
+        O(1, 7, "V")
+        YQ(1, 2)
+        Y(1, 6, "S")
+        Y(1, 1, "S")
+        O(1, 4, "V")
+        YQ(1, 0)
+        Y(1, 7, "S")
+        YQ(1, 3)
         YS(1)

@@ -48,10 +48,13 @@ def tile_dpfpfastweightwriteread_x1_kernel(tc, q, k, v, beta, s0, gq, gs, out_0,
         def load_k(b, g):
             if b not in kx:
                 kx[b] = keep.tile([P, 8, A], BF16, name="kx%d" % b)
-            nc.sync.dma_start(
-                out=kx[b][:, 4 * g : 4 * g + 4, :],
-                in_=k[b, 512 * g : 512 * g + 512, :].rearrange("(p j) a -> p j a", j=4),
-            )
+            pieces = 2 if (b, g) == (0, 0) else 1
+            n = 4 // pieces
+            for i in range(pieces):
+                nc.sync.dma_start(
+                    out=kx[b][:, 4 * g + n * i : 4 * g + n * i + n, :],
+                    in_=k[b, 512 * g : 512 * g + 512, :].rearrange("(p j) a -> p j a", j=4)[:, n * i : n * i + n, :],
+                )
 
         def load_q(b, h):
             if b not in qx:
@@ -68,6 +71,11 @@ def tile_dpfpfastweightwriteread_x1_kernel(tc, q, k, v, beta, s0, gq, gs, out_0,
         def load_s0(b):
             s0x[b] = keep.tile([P, 4, E], BF16, name="s0x%d" % b)
             nc.sync.dma_start(out=s0x[b][:], in_=s0[b].rearrange("(p j) e -> p j e", j=4))
+
+        def warm():
+            one = keep.tile([P, 1], F32, name="one")
+            nc.gpsimd.memset(one[:], 1.0)
+            nc.scalar.activation(out=one[:], in_=one[:], func=ACT.Sqrt)
 
         def consts():
             nc.gpsimd.memset(rows[:], 0.0)
@@ -95,8 +103,11 @@ def tile_dpfpfastweightwriteread_x1_kernel(tc, q, k, v, beta, s0, gq, gs, out_0,
             nc.scalar.mul(gs07[:], csm[:, :, 4], 0.7)
             nc.scalar.mul(gs32[:], csm[:, :, 4], 1.0 / 32.0)
 
-        def products(x, w):
-            nc.vector.tensor_tensor(out=w[:, :, 1:A], in0=x[:, :, 1:A], in1=x[:, :, 0 : A - 1], op=ALU.mult)
+        def products(x, w, pieces=1):
+            n = x.shape[1] // pieces
+            for i in range(pieces):
+                s = slice(n * i, n * i + n)
+                nc.vector.tensor_tensor(out=w[:, s, 1:A], in0=x[:, s, 1:A], in1=x[:, s, 0 : A - 1], op=ALU.mult)
             nc.vector.scalar_tensor_tensor(
                 out=w[:, :, 0:1], in0=x[:, :, 0:1], scalar=-1.0, in1=x[:, :, A - 1 : A], op0=ALU.mult, op1=ALU.mult
             )
@@ -115,7 +126,7 @@ def tile_dpfpfastweightwriteread_x1_kernel(tc, q, k, v, beta, s0, gq, gs, out_0,
             if b not in wk:
                 wk[b] = work.tile([P, 8, A], F32, name="wk")
             part = slice(0, 8) if g is None else slice(4 * g, 4 * g + 4)
-            products(kx[b][:, part, :], wk[b][:, part, :])
+            products(kx[b][:, part, :], wk[b][:, part, :], 2 if (b, g) == (0, 0) else 1)
 
         def WQ(b):
             uq[b] = work.tile([P, 8, A], F32, name="uq")
@@ -239,10 +250,17 @@ def tile_dpfpfastweightwriteread_x1_kernel(tc, q, k, v, beta, s0, gq, gs, out_0,
                 out=kc[b, g][:].bitcast(FP8X4), scales=ks[b, g][:], in_=kw[b, g][:].rearrange("p t h c -> p (t h c)")
             )
 
-        def S0(b, t):
+        def S0(b, t, eng):
             if b not in s0p:
                 s0p[b] = work.tile([P, 4, E], F32, name="s0p")
-            nc.scalar.activation(out=s0p[b][:, t, :], in_=s0x[b][:, t, :], func=ACT.Copy, scale=gs07[:, t : t + 1])
+            if eng == "S":
+                nc.scalar.activation(
+                    out=s0p[b][:, t, :], in_=s0x[b][:, t, :], func=ACT.Copy, scale=gs07[:, t : t + 1]
+                )
+            else:
+                nc.vector.tensor_scalar(
+                    out=s0p[b][:, t, :], in0=s0x[b][:, t, :], scalar1=gs07[:, t : t + 1], scalar2=None, op0=ALU.mult
+                )
 
         def MM(b, t):
             dd[b, t] = psum_d.tile([P, E], F32, name="d")
@@ -318,9 +336,10 @@ def tile_dpfpfastweightwriteread_x1_kernel(tc, q, k, v, beta, s0, gq, gs, out_0,
             for u in range(2):
                 nc.tensor.transpose(qt[b, n // 2][:, n % 2, u, :], words[:, u:A:2], ident[:])
 
-        def QG(b, c):
+        def QG(b, c, eng):
             qg[b, c] = work.tile([P, 2, P, 4], BF16, name="qg", align_bytes=64)
-            nc.scalar.copy(
+            move = nc.scalar.copy if eng == "S" else nc.vector.tensor_copy
+            move(
                 out=qg[b, c][:]
                 .rearrange("p c r e -> p (c r e)")
                 .bitcast(F32)
@@ -399,6 +418,7 @@ def tile_dpfpfastweightwriteread_x1_kernel(tc, q, k, v, beta, s0, gq, gs, out_0,
                     in_=ysc[b][32 * quad : 32 * quad + 4, :].bitcast(I32),
                 )
 
+        warm()
         consts()
         load_k(0, 0)
         load_small()
@@ -415,192 +435,192 @@ def tile_dpfpfastweightwriteread_x1_kernel(tc, q, k, v, beta, s0, gq, gs, out_0,
         load_v(1, 0)
         load_v(1, 1)
         load_s0(1)
-        VP(0, 0, 1)
         WK(0, 0)
         RK(0, 0)
-        MI(0)
         WK(0, 1)
         RK(0, 1)
-        ZM(0, 1)
         WQ(0)
-        WK(1)
         GA()
         gains()
-        VIP(0, 0, 1)
-        RQ(0, 1)
-        ZM(0, 0)
-        XP(0, 0)
-        WQ(1)
-        GB()
-        Z(0, 0)
         RQ(0, 0)
-        MI(1)
-        CH(0, 0)
-        Z(0, 1)
         VP(0, 0, 0)
+        RQ(0, 1)
+        WK(1)
+        GB()
+        MI(0)
+        ZM(0, 0)
+        S0(0, 0, "V")
+        ZM(0, 1)
+        VP(0, 0, 1)
+        VIP(0, 0, 1)
         VIP(0, 0, 0)
-        CH(0, 1)
-        CH(0, 2)
-        VQ(0, 0)
-        VI(0, 1, "S")
-        QF(0, 2)
-        CH(0, 3)
-        QF(0, 3)
-        KR(0, 0, "S")
-        VI(1, 0, "V")
-        QF(0, 1)
-        KI(0, 0)
-        QF(0, 0)
-        TR(0, 2)
-        TR(0, 3)
-        QG(0, 1)
+        VI(0, 1, "V")
+        WQ(1)
+        CH(0, 0)
         XP(0, 1)
-        ZM(1, 1)
-        KR(0, 1, "S")
-        KI(0, 1)
-        S0(0, 3)
-        RQ(1, 0)
-        RK(1, 0)
-        KP(0, 0)
-        KP(0, 1)
-        S0(0, 0)
-        S0(0, 1)
+        CH(0, 1)
+        Z(0, 0)
+        Z(0, 1)
+        CH(0, 2)
+        MI(1)
+        QF(0, 0)
         TR(0, 0)
-        QQ(0, 1)
-        KM(0, 1)
-        KM(0, 0)
-        KQ(0, 1)
-        KQ(0, 0)
-        TR(0, 1)
-        QG(0, 0)
-        QF(0, 4)
-        TR(0, 4)
-        VQ(0, 1)
-        MM(0, 1)
-        QF(0, 7)
-        MM(0, 2)
+        CH(0, 3)
         QF(0, 5)
-        ZM(1, 0)
+        VQ(0, 1)
+        XP(0, 0)
+        RQ(1, 0)
+        KR(0, 0, "S")
+        KR(0, 1, "S")
+        QF(0, 1)
+        QF(0, 4)
+        TR(0, 1)
+        KI(0, 0)
         TR(0, 5)
-        S0(0, 2)
-        SN(0, 1)
-        VQ(1, 0)
-        SN(0, 2)
         RQ(1, 1)
-        RK(1, 1)
-        MM(0, 0)
-        MM(0, 3)
-        Z(1, 1)
-        QF(0, 6)
-        TR(0, 6)
-        SN(0, 0)
-        TR(0, 7)
-        XP(1, 1)
-        Z(1, 0)
+        KI(0, 1)
+        S0(0, 2, "S")
+        QG(0, 0, "S")
+        VQ(0, 0)
+        QF(0, 7)
+        KP(0, 0)
+        ZM(1, 1)
+        RK(1, 0)
+        KM(0, 0)
+        KP(0, 1)
         QQ(0, 0)
+        RK(1, 1)
+        KM(0, 1)
+        KQ(0, 0)
+        ZM(1, 0)
+        KQ(0, 1)
+        TR(0, 4)
+        QF(0, 2)
+        QG(0, 2, "S")
+        QF(0, 6)
+        MM(0, 0)
+        QF(0, 3)
+        S0(0, 3, "S")
+        S0(0, 1, "S")
+        TR(0, 7)
+        SN(0, 0)
+        Z(1, 1)
+        TR(0, 6)
         CH(1, 0)
-        SN(0, 3)
-        QG(0, 2)
         QQ(0, 2)
         CH(1, 1)
+        Z(1, 0)
         CH(1, 2)
-        QG(0, 3)
-        XP(1, 0)
-        SI(0, 0)
+        TR(0, 3)
+        MM(0, 1)
+        MM(0, 2)
+        TR(0, 2)
+        SN(0, 1)
+        QG(0, 3, "S")
         QF(1, 0)
+        SN(0, 2)
         VI(1, 1, "S")
-        TR(1, 0)
         CH(1, 3)
-        KR(1, 1, "S")
-        SI(0, 1)
-        QF(1, 3)
-        TR(1, 3)
-        SQ(0)
-        QQ(0, 3)
-        QF(1, 1)
-        KI(1, 1)
-        KR(1, 0, "S")
-        Y(0, 0, "S")
-        VQ(1, 1)
-        KI(1, 0)
-        Y(0, 7, "S")
-        Y(0, 4, "S")
         QF(1, 2)
-        S0(1, 1)
-        O(0, 5, "S")
-        S0(1, 2)
-        KP(1, 1)
-        KP(1, 0)
-        Y(0, 5, "S")
-        KM(1, 1)
-        Y(0, 6, "S")
-        KM(1, 0)
-        Y(0, 3, "S")
-        TR(1, 2)
-        TR(1, 1)
+        KR(1, 1, "S")
+        MM(0, 3)
+        KR(1, 0, "S")
+        SN(0, 3)
+        QF(1, 3)
+        SI(0, 0)
+        XP(1, 1)
+        VI(1, 0, "S")
+        QF(1, 1)
+        XP(1, 0)
+        SI(0, 1)
+        S0(1, 1, "S")
+        KI(1, 0)
+        SQ(0)
+        TR(1, 3)
+        QG(0, 1, "S")
         Y(0, 1, "S")
-        KQ(1, 1)
-        KQ(1, 0)
-        S0(1, 3)
-        YQ(0, 3)
+        Y(0, 0, "S")
         O(0, 1, "S")
-        S0(1, 0)
-        QG(1, 1)
-        Y(0, 2, "S")
-        MM(1, 2)
-        QG(1, 0)
-        QF(1, 7)
-        QF(1, 4)
+        TR(1, 2)
+        TR(1, 0)
+        KI(1, 1)
+        KP(1, 0)
+        KP(1, 1)
+        S0(1, 0, "S")
+        O(0, 5, "S")
         O(0, 0, "S")
-        O(0, 4, "S")
-        YQ(0, 2)
-        SN(1, 2)
+        QQ(0, 3)
+        KM(1, 0)
+        S0(1, 3, "S")
+        VQ(1, 1)
+        QG(1, 1, "S")
+        KQ(1, 0)
+        S0(1, 2, "S")
+        KM(1, 1)
+        O(0, 7, "S")
+        Y(0, 7, "S")
+        O(0, 6, "S")
+        Y(0, 4, "S")
+        TR(1, 1)
+        VQ(1, 0)
+        KQ(1, 1)
+        QQ(0, 1)
+        MM(1, 2)
+        QF(1, 4)
+        QG(1, 0, "S")
+        MM(1, 3)
         QF(1, 5)
+        O(0, 3, "S")
+        SN(1, 2)
+        SN(1, 3)
+        QF(1, 7)
+        MM(1, 1)
+        QF(1, 6)
+        SN(1, 1)
         MM(1, 0)
         SN(1, 0)
-        MM(1, 1)
-        SN(1, 1)
-        QF(1, 6)
-        MM(1, 3)
-        SN(1, 3)
         QQ(1, 1)
         SI(1, 0)
         SI(1, 1)
-        O(0, 7, "S")
-        O(0, 2, "S")
-        YQ(0, 1)
-        SQ(1)
-        TR(1, 4)
-        TR(1, 5)
-        TR(1, 6)
-        QG(1, 2)
         QQ(1, 0)
-        QQ(1, 2)
+        O(0, 2, "S")
+        Y(0, 5, "S")
+        O(0, 4, "S")
+        Y(0, 6, "S")
+        TR(1, 6)
+        SQ(1)
+        TR(1, 5)
         TR(1, 7)
-        O(0, 3, "S")
-        O(0, 6, "S")
+        QG(1, 3, "S")
+        TR(1, 4)
+        QG(1, 2, "S")
         YQ(0, 0)
-        YS(0)
-        O(1, 1, "V")
-        QG(1, 3)
-        Y(1, 2, "S")
-        O(1, 5, "V")
-        O(1, 0, "S")
-        O(1, 2, "S")
+        YQ(0, 2)
+        Y(0, 3, "S")
+        YQ(0, 3)
+        QQ(1, 2)
+        O(1, 3, "S")
+        O(1, 1, "S")
+        O(1, 0, "V")
         QQ(1, 3)
-        Y(1, 0, "V")
-        Y(1, 3, "S")
-        O(1, 3, "V")
-        O(1, 6, "S")
-        YQ(1, 1)
-        Y(1, 5, "S")
-        Y(1, 4, "V")
-        O(1, 7, "V")
-        YQ(1, 2)
-        Y(1, 6, "S")
         Y(1, 1, "S")
+        Y(1, 3, "S")
         O(1, 4, "V")
+        Y(1, 0, "S")
+        O(1, 6, "V")
         YQ(1, 0)
+        O(1, 7, "S")
+        Y(0, 2, "V")
+        YQ(0, 1)
+        YS(0)
+        Y(1, 5, "S")
+        O(1, 5, "S")
+        Y(1, 2, "V")
+        O(1, 2, "V")
+        Y(1, 4, "S")
+        Y(1, 6, "V")
+        YQ(1, 2)
         Y(1, 7, "S")
+        YQ(1, 1)
         YQ(1, 3)
         YS(1)

from contextlib import ExitStack

import concourse.mybir as mybir
from concourse.masks import make_identity

B, T, A, E = 2, 1024, 256, 512
F = 2 * A
FLOPS = 2 * 2 * B * T * F * E

F32 = mybir.dt.float32
BF16 = mybir.dt.bfloat16
I32 = mybir.dt.int32
U32 = mybir.dt.uint32
U8 = mybir.dt.uint8
FP8X4 = mybir.dt.float8_e4m3fn_x4
ALU = mybir.AluOpType
ACT = mybir.ActivationFunctionType
P = 128


def tile_dpfpfastweightwriteread_x1_kernel(tc, q, k, v, beta, s0, gq, gs, out_0, out_1, out_2):
    nc = tc.nc

    with ExitStack() as ctx:
        keep = ctx.enter_context(tc.tile_pool(name="keep", bufs=1))
        work = ctx.enter_context(tc.tile_pool(name="work", bufs=2))
        small = ctx.enter_context(tc.tile_pool(name="small", bufs=2))
        outp = ctx.enter_context(tc.tile_pool(name="outp", bufs=6))
        psum_d = ctx.enter_context(tc.psum_pool(name="psum_d", bufs=2))
        psum_q = ctx.enter_context(tc.psum_pool(name="psum_q", bufs=2))
        psum_o = ctx.enter_context(tc.psum_pool(name="psum_o", bufs=4))
        ctx.enter_context(tc.manual_schedule())

        kx, qx, vx, s0x = {}, {}, {}, {}
        wk, uq, ss, r, ck = {}, {}, {}, {}, {}
        mi, xp, vi, vp, kr, ki, kw, kc, ks, vc, vs = {}, {}, {}, {}, {}, {}, {}, {}, {}, {}, {}
        s0p, sn, si, sc, sscale = {}, {}, {}, {}, {}
        qm, z, qf, qt, qg, qc, qs, yg, ysc, dd = {}, {}, {}, {}, {}, {}, {}, {}, {}, {}

        rows = keep.tile([P, F], BF16, name="rows")
        csm = keep.tile([P, 4, 8], BF16, name="csm")
        gqb = keep.tile([P, F], BF16, name="gqb")
        ident = keep.tile([P, P], F32, name="ident")
        ident16 = keep.tile([P, P], BF16, name="ident16")
        gs07 = keep.tile([P, 4], F32, name="gs07")
        gs32 = keep.tile([P, 4], F32, name="gs32")

        def load_k(b, g):
            if b not in kx:
                kx[b] = keep.tile([P, 8, A], BF16, name="kx%d" % b)
            pieces = 2 if (b, g) == (0, 0) else 1
            n = 4 // pieces
            for i in range(pieces):
                nc.sync.dma_start(
                    out=kx[b][:, 4 * g + n * i : 4 * g + n * i + n, :],
                    in_=k[b, 512 * g : 512 * g + 512, :].rearrange("(p j) a -> p j a", j=4)[:, n * i : n * i + n, :],
                )

        def load_q(b, h):
            if b not in qx:
                qx[b] = keep.tile([P, 8, A], BF16, name="qx%d" % b)
            nc.sync.dma_start(
                out=qx[b][:, 4 * h : 4 * h + 4, :],
                in_=q[b, 512 * h : 512 * h + 512, :].rearrange("(c p) a -> p c a", p=P),
            )

        def load_v(b, g):
            vx[b, g] = keep.tile([P, 4, E], BF16, name="vx%d%d" % (b, g))
            nc.sync.dma_start(out=vx[b, g][:], in_=v[b, 512 * g : 512 * g + 512, :].rearrange("(p j) e -> p j e", j=4))

        def load_s0(b):
            s0x[b] = keep.tile([P, 4, E], BF16, name="s0x%d" % b)
            nc.sync.dma_start(out=s0x[b][:], in_=s0[b].rearrange("(p j) e -> p j e", j=4))

        def warm():
            one = keep.tile([P, 1], F32, name="one")
            nc.gpsimd.memset(one[:], 1.0)
            nc.scalar.activation(out=one[:], in_=one[:], func=ACT.Sqrt)

        def consts():
            nc.gpsimd.memset(rows[:], 0.0)
            make_identity(nc, ident16[:])
            make_identity(nc, ident[:])

        def load_small():
            nc.scalar.dma_start(out=rows[0:4, :], in_=beta.rearrange("b (g x) -> (b g) x", g=2))
            nc.scalar.dma_start(out=rows[4:5, :], in_=gs.rearrange("(o x) -> o x", o=1))
            nc.scalar.dma_start(out=rows[5:6, :], in_=gq.rearrange("(o x) -> o x", o=1))

        def GA():
            t = psum_o.tile([P, 4, P], BF16, name="o")
            for j in range(4):
                nc.tensor.transpose(t[:, j, :], rows[:, j:F:4], ident16[:])
            nc.scalar.copy(out=csm[:], in_=t[:, :, 0:8])

        def GB():
            t = psum_o.tile([P, 4, P], BF16, name="o")
            for j in range(4):
                nc.tensor.transpose(t[:, j, :], csm[:, j, 5:6].to_broadcast([P, P]), ident16[:])
            nc.scalar.copy(out=gqb[:].rearrange("p (n j) -> p n j", j=4), in_=t[:].rearrange("p j n -> p n j"))

        def gains():
            nc.scalar.mul(gs07[:], csm[:, :, 4], 0.7)
            nc.scalar.mul(gs32[:], csm[:, :, 4], 1.0 / 32.0)

        def products(x, w, pieces=1):
            n = x.shape[1] // pieces
            for i in range(pieces):
                s = slice(n * i, n * i + n)
                nc.vector.tensor_tensor(out=w[:, s, 1:A], in0=x[:, s, 1:A], in1=x[:, s, 0 : A - 1], op=ALU.mult)
            nc.vector.scalar_tensor_tensor(
                out=w[:, :, 0:1], in0=x[:, :, 0:1], scalar=-1.0, in1=x[:, :, A - 1 : A], op0=ALU.mult, op1=ALU.mult
            )

        def squares(w, b, base):
            nc.scalar.activation(out=w, in_=w, func=ACT.Relu)
            if b not in ss:
                ss[b] = small.tile([P, 16], F32, name="ss")
            for j in range(4):
                junk = small.tile([P, A], BF16, name="junk")
                nc.scalar.activation(
                    out=junk[:], in_=w[:, j, :], func=ACT.Square, accum_out=ss[b][:, base + j : base + j + 1]
                )

        def WK(b, g=None):
            if b not in wk:
                wk[b] = work.tile([P, 8, A], F32, name="wk")
            part = slice(0, 8) if g is None else slice(4 * g, 4 * g + 4)
            products(kx[b][:, part, :], wk[b][:, part, :], 2 if (b, g) == (0, 0) else 1)

        def WQ(b):
            uq[b] = work.tile([P, 8, A], F32, name="uq")
            products(qx[b][:], uq[b][:])

        def RK(b, g):
            squares(wk[b][:, 4 * g : 4 * g + 4, :], b, 4 * g)

        def RQ(b, h):
            squares(uq[b][:, 4 * h : 4 * h + 4, :], b, 8 + 4 * h)

        def CH(b, i):
            if i == 0:
                r[b] = small.tile([P, 16], F32, name="r")
                nc.vector.tensor_scalar(
                    out=ss[b][:], in0=ss[b][:], scalar1=1.0 / F, scalar2=1e-6, op0=ALU.mult, op1=ALU.add
                )
            elif i == 1:
                nc.scalar.activation(out=r[b][:], in_=ss[b][:], func=ACT.Sqrt)
            elif i == 2:
                nc.vector.reciprocal(out=r[b][:], in_=r[b][:])
            else:
                ck[b] = small.tile([P, 8], F32, name="ck")
                nc.vector.tensor_tensor(
                    out=ck[b][:].rearrange("p (g j) -> p g j", g=2),
                    in0=r[b][:, 0:8].rearrange("p (g j) -> p g j", g=2),
                    in1=csm[:, :, 2 * b : 2 * b + 2].rearrange("p j g -> p g j"),
                    op=ALU.mult,
                )

        def MI(b):
            mi[b] = work.tile([P, 8, A], BF16, name="mi")
            nc.vector.tensor_scalar(out=mi[b][:], in0=kx[b][:], scalar1=0.0, scalar2=None, op0=ALU.is_gt)

        def XP(b, g):
            xp[b, g] = psum_d.tile([P, 4, 256], BF16, name="d")
            src = mi[b][:, 4 * g : 4 * g + 4, :].rearrange("p j (m t) -> p t m j", t=4)
            for i in range(2):
                nc.tensor.matmul(
                    out=xp[b, g][:, 2 * i : 2 * i + 2, :].rearrange("p t c -> p (t c)"),
                    lhsT=ident16[:],
                    rhs=src[:, 2 * i : 2 * i + 2],
                    start=True,
                    stop=True,
                )

        def VP(b, g, h):
            vp[b, g, h] = psum_o.tile([P, 2 * E], BF16, name="o")
            src = vx[b, g][:].rearrange("p j e -> p e j")
            for i in range(2):
                e0 = 256 * h + 128 * i
                nc.tensor.matmul(
                    out=vp[b, g, h][:, E * i : E * i + E],
                    lhsT=ident16[:],
                    rhs=src[:, e0 : e0 + 128, :],
                    start=True,
                    stop=True,
                )

        def new_vi(b, g):
            if (b, g) not in vi:
                vi[b, g] = work.tile([P, E, 4], BF16, name="vi", align_bytes=64, bufs=3)

        def VIP(b, g, h):
            new_vi(b, g)
            nc.scalar.copy(
                out=vi[b, g][:, 256 * h : 256 * h + 256, :].rearrange("p e j -> p (e j)"), in_=vp[b, g, h][:]
            )

        def VI(b, g, eng):
            new_vi(b, g)
            if eng == "S":
                nc.scalar.copy(out=vi[b, g][:], in_=vx[b, g][:].rearrange("p j e -> p e j"))
            else:
                nc.vector.tensor_copy(out=vi[b, g][:], in_=vx[b, g][:].rearrange("p j e -> p e j"))

        def VQ(b, g):
            vc[b, g] = work.tile([P, E], U32, name="vc%d" % g, align_bytes=64)
            vs[b, g] = work.tile([P, E], U8, name="vs%d" % g, align_bytes=64)
            nc.vector.quantize_mx(
                out=vc[b, g][:].bitcast(FP8X4), scales=vs[b, g][:], in_=vi[b, g][:].rearrange("p e j -> p (e j)")
            )

        def KR(b, g, eng):
            kr[b, g] = work.tile([P, 4, A], BF16, name="kr")
            for j in range(4):
                n = 4 * g + j
                if eng == "S":
                    nc.scalar.activation(
                        out=kr[b, g][:, j, :], in_=wk[b][:, n, :], func=ACT.Copy, scale=ck[b][:, n : n + 1]
                    )
                else:
                    nc.vector.tensor_scalar(
                        out=kr[b, g][:, j, :],
                        in0=wk[b][:, n, :],
                        scalar1=ck[b][:, n : n + 1],
                        scalar2=None,
                        op0=ALU.mult,
                    )

        def KI(b, g):
            ki[b, g] = work.tile([P, 4, 256], BF16, name="ki")
            nc.vector.tensor_copy(
                out=ki[b, g][:].rearrange("p t (m c) -> p m t c", c=8),
                in_=kr[b, g][:].rearrange("p j (m i t) -> p m t i j", i=2, t=4),
            )

        def KP(b, g):
            kw[b, g] = work.tile([P, 4, 2, 256], BF16, name="kw", align_bytes=64)
            nc.vector.tensor_tensor(out=kw[b, g][:, :, 0, :], in0=ki[b, g][:], in1=xp[b, g][:], op=ALU.mult)

        def KM(b, g):
            nc.vector.tensor_tensor(
                out=kw[b, g][:, :, 1, :], in0=ki[b, g][:], in1=kw[b, g][:, :, 0, :], op=ALU.subtract
            )

        def KQ(b, g):
            kc[b, g] = work.tile([P, F], U32, name="kc%d" % g, align_bytes=64)
            ks[b, g] = work.tile([P, F], U8, name="ks%d" % g, align_bytes=64)
            nc.vector.quantize_mx(
                out=kc[b, g][:].bitcast(FP8X4), scales=ks[b, g][:], in_=kw[b, g][:].rearrange("p t h c -> p (t h c)")
            )

        def S0(b, t, eng):
            if b not in s0p:
                s0p[b] = work.tile([P, 4, E], F32, name="s0p")
            if eng == "S":
                nc.scalar.activation(
                    out=s0p[b][:, t, :], in_=s0x[b][:, t, :], func=ACT.Copy, scale=gs07[:, t : t + 1]
                )
            else:
                nc.vector.tensor_scalar(
                    out=s0p[b][:, t, :], in0=s0x[b][:, t, :], scalar1=gs07[:, t : t + 1], scalar2=None, op0=ALU.mult
                )

        def MM(b, t):
            dd[b, t] = psum_d.tile([P, E], F32, name="d")
            for g in range(2):
                cols = slice(P * t, P * t + P)
                nc.tensor.matmul_mx(
                    out=dd[b, t][:],
                    lhsT=kc[b, g][:, cols].bitcast(FP8X4),
                    lhsT_scale=ks[b, g][:, cols],
                    rhs=vc[b, g][:].bitcast(FP8X4),
                    rhs_scale=vs[b, g][:],
                    start=(g == 0),
                    stop=(g == 1),
                )

        def SN(b, t):
            if b not in sn:
                sn[b] = work.tile([P, 4, E], BF16, name="sn")
            nc.vector.scalar_tensor_tensor(
                out=sn[b][:, t, :],
                in0=dd[b, t][:],
                scalar=gs32[:, t : t + 1],
                in1=s0p[b][:, t, :],
                op0=ALU.mult,
                op1=ALU.add,
            )

        def SI(b, h):
            if b not in si:
                si[b] = work.tile([P, 4, P * 4], BF16, name="si", align_bytes=64)
            nc.vector.tensor_copy(
                out=si[b][:].rearrange("p t (m c) -> p m t c", c=8)[:, 32 * h : 32 * h + 32],
                in_=sn[b][:].rearrange("p j (m i t) -> p m t i j", i=2, t=4)[:, 32 * h : 32 * h + 32],
            )

        def SQ(b):
            sc[b] = work.tile([P, E], U32, name="sc", align_bytes=64)
            sscale[b] = work.tile([P, E], U8, name="sscale", align_bytes=64)
            nc.vector.quantize_mx(
                out=sc[b][:].bitcast(FP8X4), scales=sscale[b][:], in_=si[b][:].rearrange("p t c -> p (t c)")
            )

        def ZM(b, h):
            qm[b, h] = work.tile([P, 4, 2, A], BF16, name="qm")
            src = qx[b][:, 4 * h : 4 * h + 4, :]
            nc.vector.tensor_scalar(out=qm[b, h][:, :, 0, :], in0=src, scalar1=0.0, scalar2=None, op0=ALU.is_gt)
            nc.vector.tensor_scalar(out=qm[b, h][:, :, 1, :], in0=src, scalar1=0.0, scalar2=None, op0=ALU.is_lt)

        def Z(b, h):
            z[b, h] = work.tile([P, 4, F], BF16, name="z")
            nc.vector.tensor_tensor(
                out=z[b, h][:],
                in0=qm[b, h][:].rearrange("p c h a -> p c (h a)"),
                in1=gqb[:].unsqueeze(1).to_broadcast([P, 4, F]),
                op=ALU.mult,
            )

        def QF(b, n):
            qf[b, n] = work.tile([P, F], BF16, name="qf", bufs=4)
            nc.vector.scalar_tensor_tensor(
                out=qf[b, n][:].rearrange("p (h a) -> p h a", h=2),
                in0=uq[b][:, n, :].unsqueeze(1).to_broadcast([P, 2, A]),
                scalar=r[b][:, 8 + n : 9 + n],
                in1=z[b, n // 4][:, n % 4, :].rearrange("p (h a) -> p h a", h=2),
                op0=ALU.mult,
                op1=ALU.mult,
            )

        def TR(b, n):
            if (b, n // 2) not in qt:
                qt[b, n // 2] = psum_q.tile([P, 2, 2, P], F32, name="qt")
            words = qf[b, n][:].bitcast(F32)
            for u in range(2):
                nc.tensor.transpose(qt[b, n // 2][:, n % 2, u, :], words[:, u:A:2], ident[:])

        def QG(b, c, eng):
            qg[b, c] = work.tile([P, 2, P, 4], BF16, name="qg", align_bytes=64)
            move = nc.scalar.copy if eng == "S" else nc.vector.tensor_copy
            move(
                out=qg[b, c][:]
                .rearrange("p c r e -> p (c r e)")
                .bitcast(F32)
                .rearrange("p (c r u) -> p c r u", c=2, u=2),
                in_=qt[b, c][:].rearrange("p c u r -> p c r u"),
            )

        def QQ(b, c):
            if b not in qc:
                qc[b] = work.tile([P, T], U32, name="qc", align_bytes=64)
                qs[b] = work.tile([P, T], U8, name="qs", align_bytes=64)
            tok = slice(256 * c, 256 * c + 256)
            nc.vector.quantize_mx(
                out=qc[b][:, tok].bitcast(FP8X4),
                scales=qs[b][:, tok],
                in_=qg[b, c][:].rearrange("p c r e -> p (c r e)"),
            )

        def scaled(eng, dst, src):
            if eng == "S":
                nc.scalar.activation(out=dst, in_=src, func=ACT.Copy, scale=F**-0.5)
            else:
                nc.vector.tensor_scalar(out=dst, in0=src, scalar1=F**-0.5, scalar2=None, op0=ALU.mult)

        def Y(b, n, eng):
            tok = slice(P * n, P * n + P)
            if (b, n // 2) not in yg:
                yg[b, n // 2] = work.tile([P, 256, 4], BF16, name="yg", align_bytes=64, bufs=4)
            y = psum_o.tile([P, 4, P], F32, name="o")
            for t in range(4):
                cols = slice(P * t, P * t + P)
                nc.tensor.matmul_mx(
                    out=y[:, t, :],
                    lhsT=sc[b][:, cols].bitcast(FP8X4),
                    lhsT_scale=sscale[b][:, cols],
                    rhs=qc[b][:, tok].bitcast(FP8X4),
                    rhs_scale=qs[b][:, tok],
                    start=True,
                    stop=True,
                )
            scaled(eng, yg[b, n // 2][:, P * (n % 2) : P * (n % 2) + P, :], y[:].rearrange("p t r -> p r t"))

        def O(b, n, eng):
            tok = slice(P * n, P * n + P)
            o = psum_o.tile([P, E], F32, name="o")
            nc.tensor.matmul_mx(
                out=o[:],
                lhsT=qc[b][:, tok].bitcast(FP8X4),
                lhsT_scale=qs[b][:, tok],
                rhs=sc[b][:].bitcast(FP8X4),
                rhs_scale=sscale[b][:],
                start=True,
                stop=True,
            )
            ot = outp.tile([P, E], F32, name="ot")
            scaled(eng, ot[:].rearrange("p (m t) -> p m t", t=4), o[:].rearrange("p (t m) -> p m t", t=4))
            nc.sync.dma_start(out=out_0[b, tok, :], in_=ot[:])

        def YQ(b, c):
            if b not in ysc:
                ysc[b] = work.tile([P, T], U8, name="ysc", align_bytes=64)
            tok = slice(256 * c, 256 * c + 256)
            yc = work.tile([P, 256], U32, name="yc", align_bytes=64, bufs=4)
            nc.vector.quantize_mx(
                out=yc[:].bitcast(FP8X4), scales=ysc[b][:, tok], in_=yg[b, c][:].rearrange("p r t -> p (r t)")
            )
            m0 = T * b + 256 * c
            nc.sync.dma_start(
                out=out_1[0, :, m0 : m0 + 256, :].rearrange("p m t -> p (m t)").bitcast(I32), in_=yc[:].bitcast(I32)
            )

        def YS(b):
            for quad in range(4):
                nc.sync.dma_start(
                    out=out_2[0, 4 * quad : 4 * quad + 4, T * b : T * b + T].bitcast(I32),
                    in_=ysc[b][32 * quad : 32 * quad + 4, :].bitcast(I32),
                )

        warm()
        consts()
        load_k(0, 0)
        load_small()
        load_k(0, 1)
        load_q(0, 0)
        load_q(0, 1)
        load_k(1, 0)
        load_k(1, 1)
        load_v(0, 0)
        load_v(0, 1)
        load_q(1, 0)
        load_q(1, 1)
        load_s0(0)
        load_v(1, 0)
        load_v(1, 1)
        load_s0(1)
        WK(0, 0)
        RK(0, 0)
        WK(0, 1)
        RK(0, 1)
        WQ(0)
        GA()
        gains()
        RQ(0, 0)
        VP(0, 0, 0)
        RQ(0, 1)
        WK(1)
        GB()
        MI(0)
        ZM(0, 0)
        S0(0, 0, "V")
        ZM(0, 1)
        VP(0, 0, 1)
        VIP(0, 0, 1)
        VIP(0, 0, 0)
        VI(0, 1, "V")
        WQ(1)
        CH(0, 0)
        XP(0, 1)
        CH(0, 1)
        Z(0, 0)
        Z(0, 1)
        CH(0, 2)
        MI(1)
        QF(0, 0)
        TR(0, 0)
        CH(0, 3)
        QF(0, 5)
        VQ(0, 1)
        XP(0, 0)
        RQ(1, 0)
        KR(0, 0, "S")
        KR(0, 1, "S")
        QF(0, 1)
        QF(0, 4)
        TR(0, 1)
        KI(0, 0)
        TR(0, 5)
        RQ(1, 1)
        KI(0, 1)
        S0(0, 2, "S")
        QG(0, 0, "S")
        VQ(0, 0)
        QF(0, 7)
        KP(0, 0)
        ZM(1, 1)
        RK(1, 0)
        KM(0, 0)
        KP(0, 1)
        QQ(0, 0)
        RK(1, 1)
        KM(0, 1)
        KQ(0, 0)
        ZM(1, 0)
        KQ(0, 1)
        TR(0, 4)
        QF(0, 2)
        QG(0, 2, "S")
        QF(0, 6)
        MM(0, 0)
        QF(0, 3)
        S0(0, 3, "S")
        S0(0, 1, "S")
        TR(0, 7)
        SN(0, 0)
        Z(1, 1)
        TR(0, 6)
        CH(1, 0)
        QQ(0, 2)
        CH(1, 1)
        Z(1, 0)
        CH(1, 2)
        TR(0, 3)
        MM(0, 1)
        MM(0, 2)
        TR(0, 2)
        SN(0, 1)
        QG(0, 3, "S")
        QF(1, 0)
        SN(0, 2)
        VI(1, 1, "S")
        CH(1, 3)
        QF(1, 2)
        KR(1, 1, "S")
        MM(0, 3)
        KR(1, 0, "S")
        SN(0, 3)
        QF(1, 3)
        SI(0, 0)
        XP(1, 1)
        VI(1, 0, "S")
        QF(1, 1)
        XP(1, 0)
        SI(0, 1)
        S0(1, 1, "S")
        KI(1, 0)
        SQ(0)
        TR(1, 3)
        QG(0, 1, "S")
        Y(0, 1, "S")
        Y(0, 0, "S")
        O(0, 1, "S")
        TR(1, 2)
        TR(1, 0)
        KI(1, 1)
        KP(1, 0)
        KP(1, 1)
        S0(1, 0, "S")
        O(0, 5, "S")
        O(0, 0, "S")
        QQ(0, 3)
        KM(1, 0)
        S0(1, 3, "S")
        VQ(1, 1)
        QG(1, 1, "S")
        KQ(1, 0)
        S0(1, 2, "S")
        KM(1, 1)
        O(0, 7, "S")
        Y(0, 7, "S")
        O(0, 6, "S")
        Y(0, 4, "S")
        TR(1, 1)
        VQ(1, 0)
        KQ(1, 1)
        QQ(0, 1)
        MM(1, 2)
        QF(1, 4)
        QG(1, 0, "S")
        MM(1, 3)
        QF(1, 5)
        O(0, 3, "S")
        SN(1, 2)
        SN(1, 3)
        QF(1, 7)
        MM(1, 1)
        QF(1, 6)
        SN(1, 1)
        MM(1, 0)
        SN(1, 0)
        QQ(1, 1)
        SI(1, 0)
        SI(1, 1)
        QQ(1, 0)
        O(0, 2, "S")
        Y(0, 5, "S")
        O(0, 4, "S")
        Y(0, 6, "S")
        TR(1, 6)
        SQ(1)
        TR(1, 5)
        TR(1, 7)
        QG(1, 3, "S")
        TR(1, 4)
        QG(1, 2, "S")
        YQ(0, 0)
        YQ(0, 2)
        Y(0, 3, "S")
        YQ(0, 3)
        QQ(1, 2)
        O(1, 3, "S")
        O(1, 1, "S")
        O(1, 0, "V")
        QQ(1, 3)
        Y(1, 1, "S")
        Y(1, 3, "S")
        O(1, 4, "V")
        Y(1, 0, "S")
        O(1, 6, "V")
        YQ(1, 0)
        O(1, 7, "S")
        Y(0, 2, "V")
        YQ(0, 1)
        YS(0)
        Y(1, 5, "S")
        O(1, 5, "S")
        Y(1, 2, "V")
        O(1, 2, "V")
        Y(1, 4, "S")
        Y(1, 6, "V")
        YQ(1, 2)
        Y(1, 7, "S")
        YQ(1, 1)
        YQ(1, 3)
        YS(1)
